import numpy as np, ml_dtypes
CORES = [36,164,52,180,100,228,116,244]
N = 8
BF = ml_dtypes.bfloat16
S, A, L, M, R, D = 128, 64, 32, 2, 32, 8
def steps(nx, sy):
    g = np.arange(8); s = np.zeros(8, np.int64); place = np.zeros((N * L, 8), np.int64); cnt = np.zeros((N * L, 8), np.int64)
    for i in range(N * L):
        place[i] = sy[i // L, :, i % L].astype(np.int64) * S + s
        v = nx[i // L, g, place[i]].astype(np.int64)
        s = v % S; cnt[i] = v // S
    return place, cnt
def counts(rng, uneven=False):
    k = np.argsort(rng.random((N, 8, S, A)), -1)
    w = rng.integers(0, 2, k.shape) * M if uneven else rng.integers(0, M + 1, k.shape)
    return np.ascontiguousarray(np.where(k <= M, k, w).transpose(0, 1, 3, 2))
def perms(rng):
    return np.argsort(rng.random((N, 8, A, S)), -1)
def bounds(rng):
    e = np.zeros((8, N + 1), np.int64)
    e[:, 1:N] = np.arange(1, N) * R + rng.integers(-D, D + 1, (8, N - 1)); e[:, N] = N * R - rng.integers(0, D + 1, 8)
    e[0, N] = N * R - D; e[7, N] = N * R
    return e
def draw(rng, to, ct, e, burst=False):
    n = (e[:, 1:] - e[:, :-1])[:, :, None]
    k = (np.arange(L * M) - M * rng.integers(0, L, (8, N, 1))) % (L * M) if burst else np.argsort(rng.random((8, N, L * M)), -1)
    c = np.sum((k < n).reshape(8, N, L, M), axis=-1)
    g = np.arange(8); s = np.zeros(8, np.int64); sy = np.zeros((N, 8, L), np.int32)
    for i in range(N * L):
        q = i // L; ok = ct[q][g, :, s] == c[:, q, i % L][:, None]
        a = np.argmax(np.where(ok, rng.random((8, A)), -1.0), axis=1)
        sy[q, :, i % L] = a; s = to[q][g, a, s]
    return {"nx": (ct * S + to).reshape(N, 8, A * S).astype(np.int32), "em": rng.integers(0, 64 ** M, (N, 8, A * S)).astype(np.int32), "sy": sy}
def setup_inputs(rng):
    to = np.where(rng.random((N, 8, A, 1)) < 0.125, rng.integers(0, S, (N, 8, A, S)), perms(rng))
    return draw(rng, to, counts(rng), bounds(rng))
def setup_inputs_edge(rng):
    e = bounds(rng); g = np.arange(8)[:, None]; r = np.arange(1, N)[None, :]
    e[:, 1:N] = r * R + D * np.where(g % 2 == 0, 1 - 2 * ((r + g // 2) % 2), 1 - 2 * (g // 2 % 2)); e[:, N] = N * R - D * (np.arange(8) // 4)
    return draw(rng, perms(rng), counts(rng), e)
def setup_inputs_even(rng):
    e = bounds(rng); e[:] = np.arange(N + 1) * R
    return draw(rng, perms(rng), counts(rng), e)
def setup_inputs_merge(rng):
    kind = (np.argsort(rng.random((N, 8, A)), -1) % 4)[:, :, :, None]; h = (N, 8, A, 1); s = np.arange(S)
    one = np.where(rng.random(h) < 0.5, rng.integers(0, 2, h) * (S - 1), rng.integers(0, S, h))
    to = np.where(kind == 0, one, np.where(kind == 1, s, np.where(kind == 2, (s + 1) % S, rng.integers(0, S, (N, 8, A, S)))))
    return draw(rng, to, counts(rng), bounds(rng))
def setup_inputs_spread(rng):
    to = np.minimum(np.floor(S * rng.random((N, 8, A, S)) ** 6), S - 1).astype(np.int64)
    d = draw(rng, to, counts(rng, True), bounds(rng), True)
    h = (N, 8, A * S); d["em"] = (d["em"] >> np.where(rng.random(h) < 0.5, rng.integers(0, 6 * M, h), 0)).astype(np.int32)
    return d
def check_inputs(d):
    bad = []
    for k, top in (("nx", (M + 1) * S), ("em", 64 ** M), ("sy", A)):
        if d[k].min() < 0 or d[k].max() >= top: bad.append("range of " + k)
    if bad: return bad
    place, cnt = steps(d["nx"], d["sy"])
    off = np.add.accumulate(cnt, 0)[L - 1::L] - R * np.arange(1, N + 1)[:, None]
    if (np.abs(off) > D).any(): bad.append("running totals")
    if (off[-1] > 0).any(): bad.append("whole total")
    return bad
def reference(nx, em, sy):
    place, cnt = steps(nx, sy); g = np.broadcast_to(np.arange(8), (N * L, 8)); r = (np.arange(N * L) // L)[:, None]
    e = em[r, g, place].astype(np.int64); beg = np.add.accumulate(cnt, 0) - cnt
    z = np.full((8, N * R), -1, np.int64)
    for m in range(M):
        on = cnt > m
        z[g[on], beg[on] + m] = ((e >> (6 * m)) & 63)[on]
    return {"y": np.ascontiguousarray(z.reshape(8, N, R).transpose(1, 0, 2)).astype(np.float32)}

@@ -1,0 +1,349 @@
+from concourse.bass import DstId, RemoteDMATransfer
+from concourse.mybir import AluOpType, ActivationFunctionType
+
+ALU = AluOpType
+ACTF = ActivationFunctionType
+WD = "bfloat16"
+
+SCRATCH = {
+    "syi": ("sbuf", [128, 512], "int32"),
+    "syr": ("sbuf", [128, 512], "bfloat16"),
+    "crow": ("sbuf", [128, 512], "bfloat16"),
+    "ones": ("sbuf", [128, 128], "bfloat16"),
+    "nxi": ("sbuf", [128, 512], "int32"),
+    "emi": ("sbuf", [128, 512], "int32"),
+    "nxh": ("sbuf", [128, 512], "float16"),
+    "emh": ("sbuf", [128, 512], "float16"),
+    "tb": ("sbuf", [128, 32, 32], "float16"),
+    "zz": ("sbuf", [128, 512], "bfloat16"),
+    "selm": ("sbuf", [128, 256], "float16"),
+    "sela": ("sbuf", [128, 128], "float16"),
+    "ipf": ("sbuf", [128, 8], "float32"),
+    "ipi": ("sbuf", [128, 8], "int32"),
+    "qgi": ("sbuf", [128, 8], "int32"),
+    "qgf": ("sbuf", [128, 8], "float32"),
+    "mq": ("sbuf", [128, 128], "float32"),
+    "mg": ("sbuf", [128, 128], "float32"),
+    "mi": ("sbuf", [128, 128], "float32"),
+    "rm": ("sbuf", [128, 16], "float32"),
+    "n0": ("sbuf", [128, 8], "float32"),
+    "bias": ("sbuf", [128, 24], "float32"),
+    "sg": ("sbuf", [128, 128], "float32"),
+    "b1": ("sbuf", [128, 128], "float32"),
+    "zw": ("sbuf", [128, 128], "float32"),
+    "i4": ("sbuf", [128, 128], "float32"),
+    "gcw": ("sbuf", [128, 128], WD),
+    "idm": ("sbuf", [128, 128], WD),
+    "lwc": ("sbuf", [128, 2048], WD),
+    "lwe": ("sbuf", [128, 2048], WD),
+    "wx": ("sbuf", [128, 384], WD),
+    "tri": ("sbuf", [128, 128], WD),
+    "wb": ("sbuf", [128, 128], WD),
+    "gs": ("sbuf", [128, 8], WD),
+    "iot": ("sbuf", [128, 64], "float32"),
+    "tri0": ("sbuf", [128, 128], "float32"),
+    "c1": ("sbuf", [128, 256], "float16"),
+    "cc": ("sbuf", [128, 256], "float16"),
+    "nx16": ("sbuf", [128, 256], "float16"),
+    "e16": ("sbuf", [128, 256], "float16"),
+    "oi": ("sbuf", [128, 16, 16], "int32"),
+    "oi2": ("sbuf", [128, 16, 16], "int32"),
+    "off": ("sbuf", [128, 16, 16], "uint16"),
+    "ab": ("sbuf", [128, 4096], "float32"),
+    "w0": ("sbuf", [128, 256], "float32"),
+    "w1": ("sbuf", [128, 256], "float32"),
+    "big": ("sbuf", [128, 2048], "float32"),
+    "xpb": ("sbuf", [128, 2048], "float32"),
+    "s": ("sbuf", [128, 64], "uint16"),
+    "cf": ("sbuf", [128, 256], "float32"),
+    "sf": ("sbuf", [128, 16], "float32"),
+    "pfx": ("sbuf", [128, 32], "float16"),
+    "v1": ("sbuf", [128, 192], "float32"),
+    "v2": ("sbuf", [128, 192], "float32"),
+    "cab": ("sbuf", [128, 16], WD),
+    "vi": ("sbuf", [128, 8], "int32"),
+    "ei": ("sbuf", [128, 16], "int32"),
+    "ef": ("sbuf", [128, 16], "float32"),
+    "val": ("sbuf", [128, 16], "float32"),
+    "oh": ("sbuf", [128, 384], WD),
+    "ys": ("sbuf", [128, 32], "float32"),
+    "mdo": ("dram", [128, 16], "float32"),
+    "mdi": ("dram", [8, 128, 16], "float32"),
+    "pb0": ("psum", [128, 512], "float32"),
+    "pb1": ("psum", [128, 512], "float32"),
+    "pb2": ("psum", [128, 512], "float32"),
+    "pa0": ("psum", [128, 512], "float32"),
+    "pa1": ("psum", [128, 512], "float32"),
+    "pa2": ("psum", [128, 512], "float32"),
+    "pa3": ("psum", [128, 512], "float32"),
+    "pa4": ("psum", [128, 512], "float32"),
+}
+SEMAPHORES = (["v", "a", "t", "p", "ds", "dn", "de", "mo", "yo", "lx", "lw", "lm"]
+              + ["x%d" % r for r in range(8)] + ["w%d" % r for r in range(8)]
+              + ["m%d" % r for r in range(8)] + ["ld%d" % r for r in range(8)])
+
+
+def rank_program(g, core, T, topo):
+    r = T.rank_of(core)
+    if r is None:
+        return
+    cores = T.cores
+    N = len(cores)
+    V, A, P, Y = g.vector, g.scalar, g.tensor, g.sync
+    eng = {"v": V, "a": A, "t": P, "p": g}
+    cnt = {"v": 0, "a": 0, "t": 0, "p": 0}
+    seen = {}
+
+    def wait(q, name, val):
+        if val > seen.get((q, name), 0):
+            seen[(q, name)] = val
+            (Y if q == "y" else eng[q]).wait_ge(T.sem[name], val)
+
+    def do(q, fn, *deps):
+        for name, val in deps:
+            wait(q, name, val)
+        fn().then_inc(T.sem[q], 1)
+        cnt[q] += 1
+        return (q, cnt[q])
+
+    k = 0
+    for seg in range(2):
+        q = (Y, A)[k % 2]
+        q.dma_start(T.syi[0:1, seg * 128:seg * 128 + 128], T.sy[:, 16 * seg:16 * seg + 16]).then_inc(T.sem.ds, 16)
+        k += 1
+    for h in range(2):
+        for seg in range(2):
+            q = (Y, A)[k % 2]
+            c0 = 256 + h * 128 + seg * 64
+            q.dma_start(T.syi[0:1, c0:c0 + 64], T.sy[h::2, 16 * seg:16 * seg + 16]).then_inc(T.sem.ds, 16)
+            k += 1
+    for t in range(4):
+        (Y, A)[t % 2].dma_start(T.nxi[:, 128 * t:128 * t + 128], T.nx[2 * t:2 * t + 2, :]).then_inc(T.sem.dn, 16)
+    for t in range(4):
+        (Y, A)[t % 2].dma_start(T.emi[:, 128 * t:128 * t + 128], T.em[2 * t:2 * t + 2, :]).then_inc(T.sem.de, 16)
+    DS, DN, DE = ("ds", 96), ("dn", 64), ("de", 64)
+
+    def iota(ap, pattern, base, cm):
+        return do("p", lambda: g.iota(ap, pattern, base, cm, allow_small_or_imprecise_dtypes=True))
+    iota(T.ipi[:, 0:1], [[0, 1]], 0, 1)
+    iota(T.ipf[:, 0:1], [[0, 1]], 0, 1)
+    iota(T.rm[:, 0:16], [[1, 16]], 0, 0)
+    iota(T.mq[:, :], [[0, 8], [1, 16]], 0, 0)
+    iota(T.mg[:, :], [[1, 8], [0, 16]], 0, 0)
+    pc = iota(T.mi[:, :], [[1, 128]], 0, 0)
+    iota(T.crow[:, 0:256], [[0, 8], [64, 2], [0, 16]], 0, 0)
+    pr = iota(T.crow[:, 256:512], [[0, 256]], 0, 0)
+    iota(T.iot[:, 0:32], [[1, 32]], 32 * r, 0)
+    pio = iota(T.iot[:, 32:64], [[1, 32]], 32 * r - 1, 0)
+    pz = pio
+    if r >= 2:
+        n = 256 * (r - 1)
+        iota(T.big[:, 0:n], [[0, n]], 0, 0)
+        pz = iota(T.xpb[:, 0:n], [[0, n]], 0, 0)
+
+    von = do("v", lambda: V.memset(T.ones[:, :], 1.0))
+    vz = do("v", lambda: V.memset(T.zz[:, :], 0.0))
+    do("v", lambda: V.memset(T.s[:, :], 0))
+    do("v", lambda: V.tensor_copy(T.pfx[:, 0:32], T.zz[:, 0:32]), vz)
+    do("v", lambda: V.tensor_copy(T.tb[0:64, :, 16:32], T.zz[0:64, :]), vz)
+    vtz = do("v", lambda: V.tensor_copy(T.tb[64:128, :, 0:16], T.zz[64:128, :]), vz)
+    do("v", lambda: V.tensor_scalar(T.qgi[:, 0:1], T.ipi[:, 0:1], 15, None, ALU.bitwise_and), pc)
+    do("v", lambda: V.tensor_scalar(T.qgi[:, 2:3], T.ipi[:, 0:1], 63, None, ALU.bitwise_and))
+    v = do("v", lambda: V.tensor_scalar(T.qgi[:, 1:2], T.ipi[:, 0:1], 4, None, ALU.logical_shift_right))
+    vqg = do("v", lambda: V.tensor_copy(T.qgf[:, 0:3], T.qgi[:, 0:3]), v)
+    qcol, gcol = T.qgf[:, 0:1], T.qgf[:, 1:2]
+    vrm = do("v", lambda: V.tensor_scalar(T.rm[:, :], T.rm[:, :], qcol, None, ALU.is_equal), vqg)
+    do("v", lambda: V.tensor_scalar(T.n0[:, 0:1], qcol, 0.0, None, ALU.is_gt))
+    v = do("v", lambda: V.tensor_scalar(T.n0[:, 1:2], qcol, 0.0, 4096.0, ALU.is_gt, ALU.mult))
+    do("v", lambda: V.tensor_scalar(T.sg[:, :], T.mg[:, :], gcol, None, ALU.is_equal))
+    vb1 = do("v", lambda: V.tensor_scalar(T.b1[:, :], T.mq[:, :], 0.0, 1.0 / 256, ALU.is_equal, ALU.mult))
+    do("v", lambda: V.tensor_scalar(T.i4[:, :], T.mi[:, :], T.ipf[:, 0:1], T.n0[:, 1:2], ALU.is_equal, ALU.mult), v)
+    vzw = do("v", lambda: V.tensor_tensor(T.zw[:, :], T.sg[:, :], T.b1[:, :], ALU.mult), vb1)
+    vgc = do("v", lambda: V.tensor_tensor(T.gcw[:, :], T.i4[:, :], T.zw[:, :], ALU.add), vzw)
+    vid = do("v", lambda: V.tensor_scalar(T.idm[:, :], T.mi[:, :], T.ipf[:, 0:1], None, ALU.is_equal))
+    do("v", lambda: V.tensor_scalar(T.bias[:, 0:16], T.rm[:, :], 2048.0, None, ALU.mult), vrm)
+    v = do("v", lambda: V.tensor_scalar(T.bias[:, 16:17], T.rm[:, 0:1], float(128 * (2 * r + 1)), None, ALU.mult))
+    vbi = do("v", lambda: V.tensor_tensor(T.bias[:, 16:17], T.bias[:, 16:17], T.bias[:, 15:16], ALU.add), v)
+    do("v", lambda: V.tensor_scalar(T.wx[:, 0:128], T.zw[:, :], T.rm[:, 15:16], 256.0, ALU.mult, ALU.mult))
+    vwx = do("v", lambda: V.tensor_scalar(T.wx[:, 128:256], T.zw[:, :], T.rm[:, 15:16], -32768.0, ALU.mult, ALU.mult))
+    vle = {}
+
+    def lwe(i):
+        vle[i] = do("v", lambda: V.tensor_scalar(T.lwe[:, 128 * i:128 * i + 128], T.idm[:, :], T.rm[:, i:i + 1], None, ALU.mult), vid)
+    for i in range(15, 9, -1):
+        lwe(i)
+
+    alc = {}
+    for i in range(15, -1, -1):
+        alc[i] = do("a", lambda: A.activation(T.lwc[:, 128 * i:128 * i + 128], T.gcw[:, :], ACTF.Copy, scale=T.rm[:, i:i + 1]), vgc)
+
+    do("t", lambda: P.matmul(T.pb0[:, :], T.ones[0:1, :], T.crow[0:1, :], True, False), von, pr)
+    vrow = do("v", lambda: V.tensor_copy(T.syr[0:1, :], T.syi[0:1, :]), DS)
+    tbc = do("t", lambda: P.matmul(T.pb0[:, :], T.ones[0:1, :], T.syr[0:1, :], False, True), vrow)
+    vnx = do("v", lambda: V.tensor_copy(T.nxh[:, :], T.nxi[:, :]), DN)
+    vsm = do("v", lambda: V.tensor_scalar(T.selm[:, :], T.pb0[:, 0:256], T.ipf[:, 0:1], None, ALU.is_equal), tbc)
+    txn = None
+    for seg in range(2):
+        for t in range(4):
+            txn = do("t", lambda: P.matmul(T.pb2[32 * t:32 * t + 32, 128 * seg:128 * seg + 128],
+                                           T.selm[:, 128 * seg + 32 * t:128 * seg + 32 * t + 32],
+                                           T.nxh[:, 128 * t:128 * t + 128], True, True), vsm, vnx)
+    for h in range(2):
+        for seg in range(2):
+            c0 = 256 + h * 128 + seg * 64
+            vsa = do("v", lambda: V.tensor_scalar(T.sela[64 * h:64 * h + 64, seg:128:2], T.pb0[64 * h:64 * h + 64, c0:c0 + 64],
+                                                  T.qgf[64 * h:64 * h + 64, 2:3], None, ALU.is_equal))
+    do("v", lambda: V.tensor_copy(T.tb[0:64, :, 0:16], T.nxh[0:64, :]), vnx, vtz)
+    vtb = do("v", lambda: V.tensor_copy(T.tb[64:128, :, 16:32], T.nxh[64:128, :]))
+    tof = None
+    for t in range(4):
+        for c in range(8):
+            tof = do("t", lambda: P.matmul(T.pb1[32 * t:32 * t + 32, c:256:8], T.tb[:, 8 * t + c, :],
+                                           T.sela[:, 32 * t:32 * t + 32], True, True), vtb, vsa)
+    vem = do("v", lambda: V.tensor_scalar(T.emh[:, :], T.emi[:, :], -2048, None, ALU.add), DE)
+    txe = None
+    for seg in range(2):
+        for t in range(4):
+            txe = do("t", lambda: P.matmul(T.pb0[32 * t:32 * t + 32, 128 * seg:128 * seg + 128],
+                                           T.selm[:, 128 * seg + 32 * t:128 * seg + 32 * t + 32],
+                                           T.emh[:, 128 * t:128 * t + 128], True, True), vem, vsa)
+    v = do("v", lambda: V.tensor_scalar(T.c1[:, :], T.pb2[:, 0:256], 1.0 / 128, 1024.502, ALU.mult, ALU.add), txn)
+    vcc = do("v", lambda: V.tensor_scalar(T.cc[:, :], T.c1[:, :], -1025.0, None, ALU.add), v)
+    do("v", lambda: V.tensor_copy(T.nx16[:, 0:128], T.pb2[:, 0:128]))
+    vn16 = do("v", lambda: V.tensor_scalar(T.nx16[:, 128:256], T.pb2[:, 128:256], 128.0, None, ALU.add))
+    v = do("v", lambda: V.tensor_copy(T.oi[:], T.pb1[:, 0:256]), tof)
+    v = do("v", lambda: V.tensor_scalar(T.oi2[:], T.oi[:], 127, None, ALU.bitwise_and), v)
+    ve = do("v", lambda: V.tensor_copy(T.e16[:, :], T.pb0[:, 0:256]), txe)
+    do("v", lambda: V.tensor_copy(T.off[:, :, 0:8], T.oi2[:, :, 0:8]), v)
+    vof = do("v", lambda: V.tensor_scalar(T.off[:, :, 8:16], T.oi2[:, :, 8:16], 128, None, ALU.add))
+    for i in range(9, -1, -1):
+        lwe(i)
+    vxc = do("v", lambda: V.tensor_scalar(T.wx[:, 256:384], T.idm[:, :], T.rm[:, 0:1], 4096.0, ALU.mult, ALU.mult))
+
+    pa = [T["pa%d" % b] for b in range(5)]
+    bank = [None] * 5
+    aa = {}
+    for n, i in enumerate([15, 14, 13, 12, 11, 10, 9, 8, "x", 7, 6, 5, 4, 3, 2, 1, 0]):
+        b = n % 5
+        ps = pa[b][:, 0:256]
+        deps = [vcc, ve, vn16] + ([bank[b]] if bank[b] else [])
+        if i == "x":
+            mm = [(T.lwe[:, 0:128], T.e16), (T.wx[:, 256:384], T.cc)]
+            deps += [vle[0], vxc]
+        else:
+            mm = [(T.lwc[:, 128 * i:128 * i + 128], T.cc)]
+            deps += [alc[i]]
+            if i:
+                mm.insert(0, (T.lwe[:, 128 * i:128 * i + 128], T.e16))
+                deps += [vle[i]]
+            if i == 15:
+                mm += [(T.wx[:, 0:128], T.nx16), (T.wx[:, 128:256], T.cc)]
+                deps += [vwx]
+        for j, (lh, rh) in enumerate(mm):
+            tm = do("t", lambda: P.matmul(ps, lh, rh[:, :], j == 0, j == len(mm) - 1), *deps)
+        if i == "x":
+            ax = do("a", lambda: A.activation(T.xpb[:, 256 * r:256 * r + 256], ps, ACTF.Identity, bias=T.bias[:, 0:1]), tm, vbi)
+            bank[b] = ax
+        else:
+            o = T.ab[:, 256 * i:256 * i + 256]
+            if i == 0:
+                aa[i] = do("a", lambda: A.activation(o, ps, ACTF.Identity), tm)
+            else:
+                bc = 16 if i == 15 else i
+                aa[i] = do("a", lambda: A.activation(o, ps, ACTF.Identity, bias=T.bias[:, bc:bc + 1]), tm, vbi)
+            bank[b] = aa[i]
+
+    prev, vw = T.ab[:, 256 * 15:4096], aa[15]
+    for i in range(14, -1, -1):
+        o = T.big[:, 256 * r:256 * r + 256] if i == 0 else T["w%d" % (i % 2)][:, :]
+        vw = do("v", lambda: V.tensor_tensor(o, prev.indirect(T.off[:, i, :]), T.ab[:, 256 * i:256 * i + 256], ALU.add),
+                vof, vw, aa[i])
+        prev = T["w%d" % (i % 2)][:, 0:256]
+
+    nb = [d for d in (r - 1, r + 1) if 0 <= d < N]
+
+    def send(buf_src, buf_dst, sem, lsem, dests):
+        mask = topo.mask(core, cores[dests[0]])
+        ids = []
+        for d in dests:
+            rid, pid = topo.addr(cores[d], core)
+            ids.append(DstId(rid=rid, pnc=pid))
+        g.remote_dma_fused([RemoteDMATransfer(dst_ids=ids, dma_engine_mask=mask, remote_sem=T.sem[sem],
+                                              srcs=[buf_src], dsts=[buf_dst] * len(ids))], local_sem=T.sem[lsem])
+        return len(topo.engines(core, cores[dests[0]]))
+    wait("p", *ax)
+    ne = send(T.xpb[:, 256 * r:256 * r + 256], T.xpb[:, 256 * r:256 * r + 256], "x%d" % r, "lx", nb)
+    wait("p", *vw)
+    send(T.big[:, 256 * r:256 * r + 256], T.big[:, 256 * r:256 * r + 256], "w%d" % r, "lw", nb)
+    far = list(range(r + 2, N))
+    if far:
+        wait("y", *vw)
+        Y.dma_start(T.mdo[:, :], T.big[0:128:16, 256 * r:256 * r + 256]).then_inc(T.sem.mo, 16)
+        wait("p", "mo", 16)
+        send(T.mdo[:, :], T.mdi[r], "m%d" % r, "lm", far)
+    for d in range(0, r - 1):
+        qn = "ya"[d % 2]
+        wait(qn, *pz)
+        wait(qn, "m%d" % d, ne)
+        (Y if qn == "y" else A).dma_start(T.big[0:128:16, 256 * d:256 * d + 256], T.mdi[d]).then_inc(T.sem["ld%d" % d], 16)
+
+    v = do("v", lambda: V.tensor_scalar(T.tri0[:, :], T.mq[:, :], qcol, None, ALU.is_gt))
+    do("v", lambda: V.tensor_tensor(T.tri[:, :], T.tri0[:, :], T.sg[:, :], ALU.mult), v)
+    do("v", lambda: V.tensor_scalar(T.wb[:, :], T.sg[:, :], T.rm[:, 0:1], 256.0, ALU.mult, ALU.mult))
+    vcn = do("v", lambda: V.tensor_scalar(T.gs[:, 0:8], T.mg[:, 0:128:16], gcol, None, ALU.is_equal))
+
+    kmin, kmax = max(0, 2 * r - 2), min(2 * N - 1, 2 * r + 3)
+    nk = kmax - kmin + 1
+    near = [("w%d" % d, ne) for d in nb] + [("x%d" % d, ne) for d in nb]
+    maps = [("ld%d" % d, 16) for d in range(0, r - 1)]
+    width = 256 * min(N, r + 2)
+    for name, val in near + maps:
+        wait("v", name, val)
+        wait("a", name, val)
+    wait("v", *pz)
+    wait("a", *pz)
+    wait("a", *vw)
+    win = T.big[:, 0:width]
+    vs = vcn
+    for k in range(kmax):
+        off = T.s[:, 2 * k:2 * k + 1]
+        acf = do("a", lambda: A.activation(T.cf[:, 16 * k:16 * k + 16], win.indirect(off), ACTF.Copy, scale=T.rm[:, 0:1]), vs)
+        vs = do("v", lambda: V.tensor_scalar(T.s[:, 2 * k + 2:2 * k + 18], win.indirect(off), T.rm[:, 0:1], None, ALU.mult), vs)
+    lst = T.s[:, 2 * kmin:2 * kmin + 2 * nk]
+    m = 32 * nk
+    v1 = do("v", lambda: V.tensor_scalar(T.v1[:, 0:m], win.indirect(lst), T.n0[:, 0:1], None, ALU.mult), vs)
+    vsf = do("v", lambda: V.tensor_copy(T.sf[:, 0:kmax], T.s[:, 2:2 + 2 * kmax:2]))
+    v2 = do("v", lambda: V.tensor_tensor(T.v2[:, 0:m], T.xpb[:, 0:width].indirect(lst), T.v1[:, 0:m], ALU.add), v1, ax)
+    vpx = do("v", lambda: V.tensor_tensor_scan(T.pfx[:, 1:1 + kmax], T.cf[:, 0:16 * kmax:16], T.sf[:, 0:kmax], 0.0, ALU.add, ALU.subtract),
+             vsf, acf)
+    vv = T.v2[:, 0:m:32]
+    do("v", lambda: V.tensor_scalar(T.cab[:, 0:nk], vv, 4096.0, None, ALU.is_ge), v2)
+    vca = do("v", lambda: V.tensor_scalar(T.cab[:, nk:2 * nk], vv, 8192.0, None, ALU.is_ge))
+    vi = do("v", lambda: V.tensor_copy(T.vi[:, 0:nk], vv))
+    pp = T.pb1[:, 0:nk]
+    do("t", lambda: P.matmul(pp, T.wb[:, :], T.pfx[:, kmin:kmax + 1], True, False), vpx, vof, vcn)
+    do("t", lambda: P.matmul(pp, T.tri[:, :], T.cab[:, 0:nk], False, False), vca)
+    tp = do("t", lambda: P.matmul(pp, T.tri[:, :], T.cab[:, nk:2 * nk], False, True), vca)
+    do("v", lambda: V.tensor_scalar(T.ei[:, 0:nk], T.vi[:, 0:nk], 63, None, ALU.bitwise_and), vi)
+    v = do("v", lambda: V.tensor_scalar(T.ei[:, nk:2 * nk], T.vi[:, 0:nk], 6, 63, ALU.logical_shift_right, ALU.bitwise_and))
+    v = do("v", lambda: V.tensor_scalar(T.ef[:, 0:2 * nk], T.ei[:, 0:2 * nk], 1, None, ALU.add), v)
+    vva = do("v", lambda: V.tensor_tensor(T.val[:, 0:2 * nk], T.ef[:, 0:2 * nk], T.cab[:, 0:2 * nk], ALU.mult), v, vca)
+
+    yp = T.pb2[0:8, 0:32]
+    for x in range(2 * nk):
+        mh, kk = x // nk, x % nk
+        vo = do("v", lambda: V.tensor_scalar(T.oh[:, 32 * x:32 * x + 32], T.iot[:, 32 * mh:32 * mh + 32], T.pb1[:, kk:kk + 1],
+                                             T.val[:, x:x + 1], ALU.is_equal, ALU.mult), tp, vva, pio)
+        ty = do("t", lambda: P.matmul(yp, T.gs[:, 0:8], T.oh[:, 32 * x:32 * x + 32], x == 0, x == 2 * nk - 1), vo)
+    vy = do("v", lambda: V.tensor_scalar(T.ys[0:8, :], yp, -1.0, None, ALU.add), ty)
+    wait("y", *vy)
+    Y.dma_start(T.y[:, :], T.ys[0:8, :]).then_inc(T.sem.yo, 16)
+
+    wait("y", "yo", 16)
+    wait("p", "lx", ne)
+    wait("p", "lw", ne)
+    if far:
+        wait("p", "lm", ne)
+    for name in ("v", "a", "t"):
+        wait("p", name, cnt[name])
+    wait("v", "p", cnt["p"])

@@ -3,84 +3,26 @@ from concourse.mybir import AluOpType, ActivationFunctionType
 
 ALU = AluOpType
 ACTF = ActivationFunctionType
-WD = "bfloat16"
-
-SCRATCH = {
-    "syi": ("sbuf", [128, 512], "int32"),
-    "syr": ("sbuf", [128, 512], "bfloat16"),
-    "crow": ("sbuf", [128, 512], "bfloat16"),
-    "ones": ("sbuf", [128, 128], "bfloat16"),
-    "nxi": ("sbuf", [128, 512], "int32"),
-    "emi": ("sbuf", [128, 512], "int32"),
-    "nxh": ("sbuf", [128, 512], "float16"),
-    "emh": ("sbuf", [128, 512], "float16"),
-    "tb": ("sbuf", [128, 32, 32], "float16"),
-    "zz": ("sbuf", [128, 512], "bfloat16"),
-    "selm": ("sbuf", [128, 256], "float16"),
-    "sela": ("sbuf", [128, 128], "float16"),
-    "ipf": ("sbuf", [128, 8], "float32"),
-    "ipi": ("sbuf", [128, 8], "int32"),
-    "qgi": ("sbuf", [128, 8], "int32"),
-    "qgf": ("sbuf", [128, 8], "float32"),
-    "mq": ("sbuf", [128, 128], "float32"),
-    "mg": ("sbuf", [128, 128], "float32"),
-    "mi": ("sbuf", [128, 128], "float32"),
-    "rm": ("sbuf", [128, 16], "float32"),
-    "n0": ("sbuf", [128, 8], "float32"),
-    "bias": ("sbuf", [128, 24], "float32"),
-    "sg": ("sbuf", [128, 128], "float32"),
-    "b1": ("sbuf", [128, 128], "float32"),
-    "zw": ("sbuf", [128, 128], "float32"),
-    "i4": ("sbuf", [128, 128], "float32"),
-    "gcw": ("sbuf", [128, 128], WD),
-    "idm": ("sbuf", [128, 128], WD),
-    "lwc": ("sbuf", [128, 2048], WD),
-    "lwe": ("sbuf", [128, 2048], WD),
-    "wx": ("sbuf", [128, 384], WD),
-    "tri": ("sbuf", [128, 128], WD),
-    "wb": ("sbuf", [128, 128], WD),
-    "gs": ("sbuf", [128, 8], WD),
-    "iot": ("sbuf", [128, 64], "float32"),
-    "tri0": ("sbuf", [128, 128], "float32"),
-    "c1": ("sbuf", [128, 256], "float16"),
-    "cc": ("sbuf", [128, 256], "float16"),
-    "nx16": ("sbuf", [128, 256], "float16"),
-    "e16": ("sbuf", [128, 256], "float16"),
-    "oi": ("sbuf", [128, 16, 16], "int32"),
-    "oi2": ("sbuf", [128, 16, 16], "int32"),
-    "off": ("sbuf", [128, 16, 16], "uint16"),
-    "ab": ("sbuf", [128, 4096], "float32"),
-    "w0": ("sbuf", [128, 256], "float32"),
-    "w1": ("sbuf", [128, 256], "float32"),
-    "big": ("sbuf", [128, 2048], "float32"),
-    "xpb": ("sbuf", [128, 2048], "float32"),
-    "s": ("sbuf", [128, 64], "uint16"),
-    "cf": ("sbuf", [128, 256], "float32"),
-    "sf": ("sbuf", [128, 16], "float32"),
-    "pfx": ("sbuf", [128, 32], "float16"),
-    "v1": ("sbuf", [128, 192], "float32"),
-    "v2": ("sbuf", [128, 192], "float32"),
-    "cab": ("sbuf", [128, 16], WD),
-    "vi": ("sbuf", [128, 8], "int32"),
-    "ei": ("sbuf", [128, 16], "int32"),
-    "ef": ("sbuf", [128, 16], "float32"),
-    "val": ("sbuf", [128, 16], "float32"),
-    "oh": ("sbuf", [128, 384], WD),
-    "ys": ("sbuf", [128, 32], "float32"),
-    "mdo": ("dram", [128, 16], "float32"),
-    "mdi": ("dram", [8, 128, 16], "float32"),
-    "pb0": ("psum", [128, 512], "float32"),
-    "pb1": ("psum", [128, 512], "float32"),
-    "pb2": ("psum", [128, 512], "float32"),
-    "pa0": ("psum", [128, 512], "float32"),
-    "pa1": ("psum", [128, 512], "float32"),
-    "pa2": ("psum", [128, 512], "float32"),
-    "pa3": ("psum", [128, 512], "float32"),
-    "pa4": ("psum", [128, 512], "float32"),
+F, B, H, I4, U2 = "float32", "bfloat16", "float16", "int32", "uint16"
+SBUF = {
+    I4: "syi:256 nxi:512 emi:512 ipi:8 qgi:8 v2:96 ei:16",
+    B: "syr:256 ones:128 zz:512 gcw:128 idm:128 idn:128 lwc:2048 wx:384 tri:128 wb:128 cab:16 gsv:96 oh:384",
+    H: "nxh:512 emh:512 sela:128 c1:256 cc:256 nx16:256 e16:256 pfx:32",
+    F: "ipf:8 qgf:8 mq:128 mg:128 mi:128 rm:16 rm2:16 n0:8 cu:8 bias:24 sg:128 b1:128 zw:128 i4:128 g8:96 gsr:96 l2:8 iot:64 "
+       "tri0:128 ab:4096 w0:256 w1:256 big:2048 xpb:768 cf:256 sf:16 v1:96 ef:16 val:16 ys:32",
+    U2: "uo:256 ui:2048 s:64 lst:8 gl:8",
 }
-SEMAPHORES = (["v", "a", "t", "p", "ds", "dn", "de", "mo", "yo", "lx", "lw", "lm"]
-              + ["x%d" % r for r in range(8)] + ["w%d" % r for r in range(8)]
-              + ["m%d" % r for r in range(8)] + ["ld%d" % r for r in range(8)])
+SCRATCH = {w.split(":")[0]: ("sbuf", [128, int(w.split(":")[1])], d) for d, ws in SBUF.items() for w in ws.split()}
+SCRATCH.update({
+    "selm": ("sbuf", [128, 8, 32], H), "tb": ("sbuf", [128, 32, 32], H),
+    "oi": ("sbuf", [128, 32, 8], I4), "oi2": ("sbuf", [128, 32, 8], I4),
+    "off": ("sbuf", [128, 16, 16], U2),
+    "mdo": ("dram", [128, 16], F), "mdi": ("dram", [8, 128, 16], F),
+    "xdo": ("dram", [128, 16], F), "xdi": ("dram", [8, 128, 16], F),
+})
+SCRATCH.update({n: ("psum", [128, 512], F) for n in "pb0 pb1 pb2 pa0 pa1 pa2 pa3 pa4".split()})
+SEMAPHORES = ("v a t p ds dn de mo xo yo lx lw lm".split()
+              + [s + str(r) for s in ("x", "w", "m", "ld", "lx") for r in range(8)])
 
 
 def rank_program(g, core, T, topo):
@@ -90,14 +32,17 @@ def rank_program(g, core, T, topo):
     cores = T.cores
     N = len(cores)
     V, A, P, Y = g.vector, g.scalar, g.tensor, g.sync
-    eng = {"v": V, "a": A, "t": P, "p": g}
+    eng = {"v": V, "a": A, "t": P, "p": g, "y": Y}
     cnt = {"v": 0, "a": 0, "t": 0, "p": 0}
     seen = {}
+    nb = [d for d in (r - 1, r + 1) if 0 <= d < N]
+    bl = max(0, r - 1)
+    br = min(N, r + 2)
 
     def wait(q, name, val):
         if val > seen.get((q, name), 0):
             seen[(q, name)] = val
-            (Y if q == "y" else eng[q]).wait_ge(T.sem[name], val)
+            eng[q].wait_ge(T.sem[name], val)
 
     def do(q, fn, *deps):
         for name, val in deps:
@@ -106,161 +51,154 @@ def rank_program(g, core, T, topo):
         cnt[q] += 1
         return (q, cnt[q])
 
-    k = 0
-    for seg in range(2):
-        q = (Y, A)[k % 2]
-        q.dma_start(T.syi[0:1, seg * 128:seg * 128 + 128], T.sy[:, 16 * seg:16 * seg + 16]).then_inc(T.sem.ds, 16)
-        k += 1
+    def ts(out, in0, s1, s2, op0, *op1, dep=()):
+        return do("v", lambda: V.tensor_scalar(out, in0, s1, s2, op0, *op1), *dep)
+
+    def tt(out, in0, in1, op, dep=()):
+        return do("v", lambda: V.tensor_tensor(out, in0, in1, op), *dep)
+
+    def cp(out, in_, dep=()):
+        return do("v", lambda: V.tensor_copy(out, in_), *dep)
+
+    def mm(out, lh, rh, start, stop, dep=()):
+        return do("t", lambda: P.matmul(out, lh, rh, start, stop), *dep)
+
+    def act(out, in_, func, dep=(), **kw):
+        return do("a", lambda: A.activation(out, in_, func, **kw), *dep)
+
+    def blk(buf, d, base=0):
+        return buf[:, 256 * (d - base):256 * (d - base) + 256]
+
     for h in range(2):
-        for seg in range(2):
-            q = (Y, A)[k % 2]
-            c0 = 256 + h * 128 + seg * 64
-            q.dma_start(T.syi[0:1, c0:c0 + 64], T.sy[h::2, 16 * seg:16 * seg + 16]).then_inc(T.sem.ds, 16)
-            k += 1
+        (Y, A)[h].dma_start(T.syi[0:1, 128 * h:128 * h + 128], T.sy[h::2, :]).then_inc(T.sem.ds, 16)
     for t in range(4):
         (Y, A)[t % 2].dma_start(T.nxi[:, 128 * t:128 * t + 128], T.nx[2 * t:2 * t + 2, :]).then_inc(T.sem.dn, 16)
     for t in range(4):
         (Y, A)[t % 2].dma_start(T.emi[:, 128 * t:128 * t + 128], T.em[2 * t:2 * t + 2, :]).then_inc(T.sem.de, 16)
-    DS, DN, DE = ("ds", 96), ("dn", 64), ("de", 64)
+    DS, DN, DE = ("ds", 32), ("dn", 64), ("de", 64)
 
     def iota(ap, pattern, base, cm):
         return do("p", lambda: g.iota(ap, pattern, base, cm, allow_small_or_imprecise_dtypes=True))
     iota(T.ipi[:, 0:1], [[0, 1]], 0, 1)
     iota(T.ipf[:, 0:1], [[0, 1]], 0, 1)
-    iota(T.rm[:, 0:16], [[1, 16]], 0, 0)
+    pq = iota(T.rm[:, 0:16], [[1, 16]], 0, 0)
     iota(T.mq[:, :], [[0, 8], [1, 16]], 0, 0)
     iota(T.mg[:, :], [[1, 8], [0, 16]], 0, 0)
     pc = iota(T.mi[:, :], [[1, 128]], 0, 0)
-    iota(T.crow[:, 0:256], [[0, 8], [64, 2], [0, 16]], 0, 0)
-    pr = iota(T.crow[:, 256:512], [[0, 256]], 0, 0)
     iota(T.iot[:, 0:32], [[1, 32]], 32 * r, 0)
-    pio = iota(T.iot[:, 32:64], [[1, 32]], 32 * r - 1, 0)
-    pz = pio
+    iota(T.iot[:, 32:64], [[1, 32]], 32 * r - 1, 0)
+    iota(T.l2[:, 0:6], [[2, 6]], 0, 0)
+    pio = iota(T.g8[:, :], [[0, 12], [1, 8]], 0, 0)
+    for d in nb:
+        px = iota(blk(T.xpb, d, bl), [[0, 256]], 0, 0)
+    pz = px
     if r >= 2:
-        n = 256 * (r - 1)
-        iota(T.big[:, 0:n], [[0, n]], 0, 0)
-        pz = iota(T.xpb[:, 0:n], [[0, n]], 0, 0)
+        pz = iota(T.big[:, 0:256 * bl], [[0, 256 * bl]], 0, 0)
 
     von = do("v", lambda: V.memset(T.ones[:, :], 1.0))
     vz = do("v", lambda: V.memset(T.zz[:, :], 0.0))
-    do("v", lambda: V.memset(T.s[:, :], 0))
-    do("v", lambda: V.tensor_copy(T.pfx[:, 0:32], T.zz[:, 0:32]), vz)
-    do("v", lambda: V.tensor_copy(T.tb[0:64, :, 16:32], T.zz[0:64, :]), vz)
-    vtz = do("v", lambda: V.tensor_copy(T.tb[64:128, :, 0:16], T.zz[64:128, :]), vz)
-    do("v", lambda: V.tensor_scalar(T.qgi[:, 0:1], T.ipi[:, 0:1], 15, None, ALU.bitwise_and), pc)
-    do("v", lambda: V.tensor_scalar(T.qgi[:, 2:3], T.ipi[:, 0:1], 63, None, ALU.bitwise_and))
-    v = do("v", lambda: V.tensor_scalar(T.qgi[:, 1:2], T.ipi[:, 0:1], 4, None, ALU.logical_shift_right))
-    vqg = do("v", lambda: V.tensor_copy(T.qgf[:, 0:3], T.qgi[:, 0:3]), v)
-    qcol, gcol = T.qgf[:, 0:1], T.qgf[:, 1:2]
-    vrm = do("v", lambda: V.tensor_scalar(T.rm[:, :], T.rm[:, :], qcol, None, ALU.is_equal), vqg)
-    do("v", lambda: V.tensor_scalar(T.n0[:, 0:1], qcol, 0.0, None, ALU.is_gt))
-    v = do("v", lambda: V.tensor_scalar(T.n0[:, 1:2], qcol, 0.0, 4096.0, ALU.is_gt, ALU.mult))
-    do("v", lambda: V.tensor_scalar(T.sg[:, :], T.mg[:, :], gcol, None, ALU.is_equal))
-    vb1 = do("v", lambda: V.tensor_scalar(T.b1[:, :], T.mq[:, :], 0.0, 1.0 / 256, ALU.is_equal, ALU.mult))
-    do("v", lambda: V.tensor_scalar(T.i4[:, :], T.mi[:, :], T.ipf[:, 0:1], T.n0[:, 1:2], ALU.is_equal, ALU.mult), v)
-    vzw = do("v", lambda: V.tensor_tensor(T.zw[:, :], T.sg[:, :], T.b1[:, :], ALU.mult), vb1)
-    vgc = do("v", lambda: V.tensor_tensor(T.gcw[:, :], T.i4[:, :], T.zw[:, :], ALU.add), vzw)
-    vid = do("v", lambda: V.tensor_scalar(T.idm[:, :], T.mi[:, :], T.ipf[:, 0:1], None, ALU.is_equal))
-    do("v", lambda: V.tensor_scalar(T.bias[:, 0:16], T.rm[:, :], 2048.0, None, ALU.mult), vrm)
-    v = do("v", lambda: V.tensor_scalar(T.bias[:, 16:17], T.rm[:, 0:1], float(128 * (2 * r + 1)), None, ALU.mult))
-    vbi = do("v", lambda: V.tensor_tensor(T.bias[:, 16:17], T.bias[:, 16:17], T.bias[:, 15:16], ALU.add), v)
-    do("v", lambda: V.tensor_scalar(T.wx[:, 0:128], T.zw[:, :], T.rm[:, 15:16], 256.0, ALU.mult, ALU.mult))
-    vwx = do("v", lambda: V.tensor_scalar(T.wx[:, 128:256], T.zw[:, :], T.rm[:, 15:16], -32768.0, ALU.mult, ALU.mult))
-    vle = {}
+    ts(T.qgi[:, 0:1], T.ipi[:, 0:1], 15, None, ALU.bitwise_and, dep=[pq])
+    ts(T.qgi[:, 2:3], T.ipi[:, 0:1], 63, None, ALU.bitwise_and)
+    v = ts(T.qgi[:, 1:2], T.ipi[:, 0:1], 4, None, ALU.logical_shift_right)
+    vqg = cp(T.qgf[:, 0:3], T.qgi[:, 0:3], dep=[v])
+    qcol, gcol, pcol, m0 = T.qgf[:, 0:1], T.qgf[:, 1:2], T.ipf[:, 0:1], T.rm[:, 0:1]
+    vrm = ts(T.rm[:, :], T.rm[:, :], qcol, None, ALU.is_equal, dep=[vqg])
+    ts(T.n0[:, 0:1], qcol, 0.0, None, ALU.is_gt)
+    vn0 = ts(T.n0[:, 1:2], qcol, 0.0, 4096.0, ALU.is_gt, ALU.mult)
+    ts(T.sg[:, :], T.mg[:, :], gcol, None, ALU.is_equal, dep=[pc])
+    vb1 = ts(T.b1[:, :], T.mq[:, :], 0.0, 1.0 / 256, ALU.is_equal, ALU.mult)
+    ts(T.i4[:, :], T.mi[:, :], pcol, T.n0[:, 1:2], ALU.is_equal, ALU.mult, dep=[vn0])
+    vzw = tt(T.zw[:, :], T.sg[:, :], T.b1[:, :], ALU.mult, dep=[vb1])
+    vgc = tt(T.gcw[:, :], T.i4[:, :], T.zw[:, :], ALU.add, dep=[vzw])
+    cp(T.selm[0:64, :, 16:32], T.zz[0:64, 0:128], dep=[vz])
+    cp(T.selm[64:128, :, 0:16], T.zz[64:128, 0:128])
+    cp(T.tb[0:64, :, 16:32], T.zz[0:64, :])
+    cp(T.tb[64:128, :, 0:16], T.zz[64:128, :])
 
-    def lwe(i):
-        vle[i] = do("v", lambda: V.tensor_scalar(T.lwe[:, 128 * i:128 * i + 128], T.idm[:, :], T.rm[:, i:i + 1], None, ALU.mult), vid)
-    for i in range(15, 9, -1):
-        lwe(i)
+    vrow = cp(T.syr[0:1, :], T.syi[0:1, :], dep=[DS])
+    tbc = mm(T.pb0[:, 0:256], T.ones[0:1, :], T.syr[0:1, :], True, True, dep=[von, vrow])
+    ts(T.idm[:, :], T.mi[:, :], pcol, None, ALU.is_equal)
+    ts(T.idn[:, :], T.mi[:, :], pcol, T.n0[:, 0:1], ALU.is_equal, ALU.mult)
+    ts(T.rm2[:, :], T.rm[:, :], m0, None, ALU.max, dep=[vrm])
+    ts(T.bias[:, 0:16], T.rm[:, :], 2048.0, None, ALU.mult)
+    hs = [slice(0, 64), slice(64, 128)]
+    for h in range(2):
+        vsm = ts(T.selm[hs[h], :, 16 * h:16 * h + 16], T.pb0[hs[h], 128 * h:128 * h + 128], T.qgf[hs[h], 2:3], None, ALU.is_equal, dep=[tbc])
+    for h in range(2):
+        vsa = ts(T.sela[hs[h], :], T.pb0[hs[h], 128 * h:128 * h + 128], T.qgf[hs[h], 2:3], None, ALU.is_equal)
+
+    def pick(out, tab, dep):
+        for seg in range(2):
+            for t in range(4):
+                x = mm(out[32 * t:32 * t + 32, 128 * seg:128 * seg + 128], T.selm[:, 2 * t + seg, :], tab[:, 128 * t:128 * t + 128],
+                       True, True, dep=dep)
+        return x
+    vnx = cp(T.nxh[:, :], T.nxi[:, :], dep=[DN])
+    txn = pick(T.pb2, T.nxh, [vsm, vnx])
+    cp(T.tb[0:64, :, 0:16], T.nxh[0:64, :], dep=[vnx])
+    vtb = cp(T.tb[64:128, :, 16:32], T.nxh[64:128, :])
+    vem = ts(T.emh[:, :], T.emi[:, :], -2048, None, ALU.add, dep=[DE])
+    txe = pick(T.pb0, T.emh, [vem, vsa])
+    for t in range(4):
+        for c in range(8):
+            tof = mm(T.pb1[32 * t:32 * t + 32, c:256:8], T.tb[:, 8 * t + c, :], T.sela[:, 32 * t:32 * t + 32], True, True, dep=[vtb, vsa])
+    v = ts(T.c1[:, :], T.pb2[:, 0:256], 1.0 / 128, 1024.502, ALU.mult, ALU.add, dep=[txn])
+    vcc = ts(T.cc[:, :], T.c1[:, :], -1025.0, None, ALU.add, dep=[v])
+    cp(T.nx16[:, 0:128], T.pb2[:, 0:128])
+    vn16 = ts(T.nx16[:, 128:256], T.pb2[:, 128:256], 128.0, None, ALU.add)
+    v = ts(T.bias[:, 16:17], m0, float(128 * (2 * r + 1)), None, ALU.mult)
+    ts(T.wx[:, 0:128], T.zw[:, :], T.rm[:, 15:16], 256.0, ALU.mult, ALU.mult)
+    vwx = ts(T.wx[:, 128:256], T.zw[:, :], T.rm[:, 15:16], -32768.0, ALU.mult, ALU.mult)
+    vbi = tt(T.bias[:, 17:18], T.bias[:, 16:17], T.bias[:, 15:16], ALU.add, dep=[v])
+    ve = cp(T.e16[:, :], T.pb0[:, 0:256], dep=[txe])
+    vxc = ts(T.wx[:, 256:384], T.mi[:, :], pcol, 4096.0, ALU.is_equal, ALU.mult)
+    ts(T.cu[:, 0:1], m0, 255.0, 1.0, ALU.mult, ALU.add)
+    ts(T.cu[:, 1:2], m0, -255.0 / 256, 1.0, ALU.mult, ALU.add)
+    for j, d in enumerate(nb):
+        vcu = ts(T.cu[:, 2 + j:3 + j], m0, float(128 * (2 * d + 1)), None, ALU.mult)
+    v = cp(T.oi[:], T.pb1[:, 0:256], dep=[tof])
+    v = ts(T.oi2[:], T.oi[:], 127, None, ALU.bitwise_and, dep=[v])
+    cp(T.off[:, :, 0:8], T.oi2[:, 0:16, :], dep=[v])
+    vof = ts(T.off[:, :, 8:16], T.oi2[:, 16:32, :], 128, None, ALU.add)
 
     alc = {}
     for i in range(15, -1, -1):
-        alc[i] = do("a", lambda: A.activation(T.lwc[:, 128 * i:128 * i + 128], T.gcw[:, :], ACTF.Copy, scale=T.rm[:, i:i + 1]), vgc)
-
-    do("t", lambda: P.matmul(T.pb0[:, :], T.ones[0:1, :], T.crow[0:1, :], True, False), von, pr)
-    vrow = do("v", lambda: V.tensor_copy(T.syr[0:1, :], T.syi[0:1, :]), DS)
-    tbc = do("t", lambda: P.matmul(T.pb0[:, :], T.ones[0:1, :], T.syr[0:1, :], False, True), vrow)
-    vnx = do("v", lambda: V.tensor_copy(T.nxh[:, :], T.nxi[:, :]), DN)
-    vsm = do("v", lambda: V.tensor_scalar(T.selm[:, :], T.pb0[:, 0:256], T.ipf[:, 0:1], None, ALU.is_equal), tbc)
-    txn = None
-    for seg in range(2):
-        for t in range(4):
-            txn = do("t", lambda: P.matmul(T.pb2[32 * t:32 * t + 32, 128 * seg:128 * seg + 128],
-                                           T.selm[:, 128 * seg + 32 * t:128 * seg + 32 * t + 32],
-                                           T.nxh[:, 128 * t:128 * t + 128], True, True), vsm, vnx)
-    for h in range(2):
-        for seg in range(2):
-            c0 = 256 + h * 128 + seg * 64
-            vsa = do("v", lambda: V.tensor_scalar(T.sela[64 * h:64 * h + 64, seg:128:2], T.pb0[64 * h:64 * h + 64, c0:c0 + 64],
-                                                  T.qgf[64 * h:64 * h + 64, 2:3], None, ALU.is_equal))
-    do("v", lambda: V.tensor_copy(T.tb[0:64, :, 0:16], T.nxh[0:64, :]), vnx, vtz)
-    vtb = do("v", lambda: V.tensor_copy(T.tb[64:128, :, 16:32], T.nxh[64:128, :]))
-    tof = None
-    for t in range(4):
-        for c in range(8):
-            tof = do("t", lambda: P.matmul(T.pb1[32 * t:32 * t + 32, c:256:8], T.tb[:, 8 * t + c, :],
-                                           T.sela[:, 32 * t:32 * t + 32], True, True), vtb, vsa)
-    vem = do("v", lambda: V.tensor_scalar(T.emh[:, :], T.emi[:, :], -2048, None, ALU.add), DE)
-    txe = None
-    for seg in range(2):
-        for t in range(4):
-            txe = do("t", lambda: P.matmul(T.pb0[32 * t:32 * t + 32, 128 * seg:128 * seg + 128],
-                                           T.selm[:, 128 * seg + 32 * t:128 * seg + 32 * t + 32],
-                                           T.emh[:, 128 * t:128 * t + 128], True, True), vem, vsa)
-    v = do("v", lambda: V.tensor_scalar(T.c1[:, :], T.pb2[:, 0:256], 1.0 / 128, 1024.502, ALU.mult, ALU.add), txn)
-    vcc = do("v", lambda: V.tensor_scalar(T.cc[:, :], T.c1[:, :], -1025.0, None, ALU.add), v)
-    do("v", lambda: V.tensor_copy(T.nx16[:, 0:128], T.pb2[:, 0:128]))
-    vn16 = do("v", lambda: V.tensor_scalar(T.nx16[:, 128:256], T.pb2[:, 128:256], 128.0, None, ALU.add))
-    v = do("v", lambda: V.tensor_copy(T.oi[:], T.pb1[:, 0:256]), tof)
-    v = do("v", lambda: V.tensor_scalar(T.oi2[:], T.oi[:], 127, None, ALU.bitwise_and), v)
-    ve = do("v", lambda: V.tensor_copy(T.e16[:, :], T.pb0[:, 0:256]), txe)
-    do("v", lambda: V.tensor_copy(T.off[:, :, 0:8], T.oi2[:, :, 0:8]), v)
-    vof = do("v", lambda: V.tensor_scalar(T.off[:, :, 8:16], T.oi2[:, :, 8:16], 128, None, ALU.add))
-    for i in range(9, -1, -1):
-        lwe(i)
-    vxc = do("v", lambda: V.tensor_scalar(T.wx[:, 256:384], T.idm[:, :], T.rm[:, 0:1], 4096.0, ALU.mult, ALU.mult))
+        alc[i] = act(T.lwc[:, 128 * i:128 * i + 128], T.gcw[:, :], ACTF.Copy, scale=T.rm[:, i:i + 1], dep=[vgc])
 
     pa = [T["pa%d" % b] for b in range(5)]
     bank = [None] * 5
     aa = {}
-    for n, i in enumerate([15, 14, 13, 12, 11, 10, 9, 8, "x", 7, 6, 5, 4, 3, 2, 1, 0]):
+    for n, i in enumerate([15, 14, 13, 12, 11, "x", 10, 9, 8, 7, 6, 5, 4, 3, 2, 1, 0]):
         b = n % 5
         ps = pa[b][:, 0:256]
-        deps = [vcc, ve, vn16] + ([bank[b]] if bank[b] else [])
+        deps = [vcc, ve, vn16, vwx] + ([bank[b]] if bank[b] else [])
         if i == "x":
-            mm = [(T.lwe[:, 0:128], T.e16), (T.wx[:, 256:384], T.cc)]
-            deps += [vle[0], vxc]
+            ms = [(T.idm[:, :], T.e16), (T.wx[:, 256:384], T.cc)]
+            deps += [vxc]
+            o, kw = blk(T.xpb, r, bl), dict(scale=m0, bias=T.bias[:, 0:1])
         else:
-            mm = [(T.lwc[:, 128 * i:128 * i + 128], T.cc)]
+            ms = [(T.lwc[:, 128 * i:128 * i + 128], T.cc)]
             deps += [alc[i]]
-            if i:
-                mm.insert(0, (T.lwe[:, 128 * i:128 * i + 128], T.e16))
-                deps += [vle[i]]
-            if i == 15:
-                mm += [(T.wx[:, 0:128], T.nx16), (T.wx[:, 128:256], T.cc)]
-                deps += [vwx]
-        for j, (lh, rh) in enumerate(mm):
-            tm = do("t", lambda: P.matmul(ps, lh, rh[:, :], j == 0, j == len(mm) - 1), *deps)
-        if i == "x":
-            ax = do("a", lambda: A.activation(T.xpb[:, 256 * r:256 * r + 256], ps, ACTF.Identity, bias=T.bias[:, 0:1]), tm, vbi)
-            bank[b] = ax
-        else:
             o = T.ab[:, 256 * i:256 * i + 256]
-            if i == 0:
-                aa[i] = do("a", lambda: A.activation(o, ps, ACTF.Identity), tm)
+            if i:
+                ms.append((T.idn[:, :], T.e16))
+                bc = 17 if i == 15 else i
+                kw = dict(scale=T.rm2[:, i:i + 1], bias=T.bias[:, bc:bc + 1])
             else:
-                bc = 16 if i == 15 else i
-                aa[i] = do("a", lambda: A.activation(o, ps, ACTF.Identity, bias=T.bias[:, bc:bc + 1]), tm, vbi)
-            bank[b] = aa[i]
+                kw = dict(scale=m0)
+            if i == 15:
+                ms += [(T.wx[:, 0:128], T.nx16), (T.wx[:, 128:256], T.cc)]
+        for j, (lh, rh) in enumerate(ms):
+            tm = mm(ps, lh, rh[:, :], j == 0, j == len(ms) - 1, dep=deps)
+        bank[b] = aa[i] = act(o, ps, ACTF.Identity, dep=[tm, vbi], **kw)
+    ax = aa["x"]
 
     prev, vw = T.ab[:, 256 * 15:4096], aa[15]
     for i in range(14, -1, -1):
-        o = T.big[:, 256 * r:256 * r + 256] if i == 0 else T["w%d" % (i % 2)][:, :]
-        vw = do("v", lambda: V.tensor_tensor(o, prev.indirect(T.off[:, i, :]), T.ab[:, 256 * i:256 * i + 256], ALU.add),
-                vof, vw, aa[i])
+        o = blk(T.big, r) if i == 0 else T["w%d" % (i % 2)][:, :]
+        vw = tt(o, prev.indirect(T.off[:, i, :]), T.ab[:, 256 * i:256 * i + 256], ALU.add, dep=[vof, vw, aa[i]])
         prev = T["w%d" % (i % 2)][:, 0:256]
-
-    nb = [d for d in (r - 1, r + 1) if 0 <= d < N]
+    vu = ts(T.uo[:, :], blk(T.big, r), T.bias[:, 16:17], T.cu[:, 0:1], ALU.subtract, ALU.mult, dep=[vw, vcu])
 
     def send(buf_src, buf_dst, sem, lsem, dests):
         mask = topo.mask(core, cores[dests[0]])
@@ -271,71 +209,83 @@ def rank_program(g, core, T, topo):
         g.remote_dma_fused([RemoteDMATransfer(dst_ids=ids, dma_engine_mask=mask, remote_sem=T.sem[sem],
                                               srcs=[buf_src], dsts=[buf_dst] * len(ids))], local_sem=T.sem[lsem])
         return len(topo.engines(core, cores[dests[0]]))
-    wait("p", *ax)
-    ne = send(T.xpb[:, 256 * r:256 * r + 256], T.xpb[:, 256 * r:256 * r + 256], "x%d" % r, "lx", nb)
-    wait("p", *vw)
-    send(T.big[:, 256 * r:256 * r + 256], T.big[:, 256 * r:256 * r + 256], "w%d" % r, "lw", nb)
+    wait("y", *ax)
+    Y.dma_start(T.xdo[:, :], blk(T.xpb, r, bl)[0:128:16, :]).then_inc(T.sem.xo, 16)
+    wait("p", "xo", 16)
+    ne = send(T.xdo[:, :], T.xdi[r], "x%d" % r, "lx", nb)
     far = list(range(r + 2, N))
     if far:
         wait("y", *vw)
-        Y.dma_start(T.mdo[:, :], T.big[0:128:16, 256 * r:256 * r + 256]).then_inc(T.sem.mo, 16)
+        Y.dma_start(T.mdo[:, :], blk(T.big, r)[0:128:16, :]).then_inc(T.sem.mo, 16)
+    wait("p", *vu)
+    send(T.uo[:, :], blk(T.ui, r), "w%d" % r, "lw", nb)
+    if far:
         wait("p", "mo", 16)
         send(T.mdo[:, :], T.mdi[r], "m%d" % r, "lm", far)
+    for d in nb:
+        wait("a", *px)
+        wait("a", "x%d" % d, ne)
+        A.dma_start(blk(T.xpb, d, bl)[0:128:16, :], T.xdi[d]).then_inc(T.sem["lx%d" % d], 16)
     for d in range(0, r - 1):
         qn = "ya"[d % 2]
         wait(qn, *pz)
         wait(qn, "m%d" % d, ne)
-        (Y if qn == "y" else A).dma_start(T.big[0:128:16, 256 * d:256 * d + 256], T.mdi[d]).then_inc(T.sem["ld%d" % d], 16)
-
-    v = do("v", lambda: V.tensor_scalar(T.tri0[:, :], T.mq[:, :], qcol, None, ALU.is_gt))
-    do("v", lambda: V.tensor_tensor(T.tri[:, :], T.tri0[:, :], T.sg[:, :], ALU.mult), v)
-    do("v", lambda: V.tensor_scalar(T.wb[:, :], T.sg[:, :], T.rm[:, 0:1], 256.0, ALU.mult, ALU.mult))
-    vcn = do("v", lambda: V.tensor_scalar(T.gs[:, 0:8], T.mg[:, 0:128:16], gcol, None, ALU.is_equal))
+        eng[qn].dma_start(blk(T.big, d)[0:128:16, :], T.mdi[d]).then_inc(T.sem["ld%d" % d], 16)
 
     kmin, kmax = max(0, 2 * r - 2), min(2 * N - 1, 2 * r + 3)
     nk = kmax - kmin + 1
-    near = [("w%d" % d, ne) for d in nb] + [("x%d" % d, ne) for d in nb]
-    maps = [("ld%d" % d, 16) for d in range(0, r - 1)]
-    width = 256 * min(N, r + 2)
-    for name, val in near + maps:
-        wait("v", name, val)
-        wait("a", name, val)
+    do("v", lambda: V.memset(T.s[:, :], 0))
+    cp(T.pfx[:, 0:32], T.zz[:, 0:32])
+    v = ts(T.tri0[:, :], T.mq[:, :], qcol, None, ALU.is_gt)
+    tt(T.tri[:, :], T.tri0[:, :], T.sg[:, :], ALU.mult, dep=[v])
+    ts(T.wb[:, :], T.sg[:, :], m0, 256.0, ALU.mult, ALU.mult)
+    v = ts(T.n0[:, 2:3], qcol, 8.0, None, ALU.is_ge)
+    ts(T.gl[:, 0:6], T.l2[:, 0:6], T.n0[:, 2:3], None, ALU.add, dep=[v, pio])
+    vcn = ts(T.gsr[:, :], T.g8[:, :], gcol, None, ALU.is_equal)
+    for j, d in enumerate(nb):
+        vcv = ts(blk(T.big, d), blk(T.ui, d), T.cu[:, 1:2], T.cu[:, 2 + j:3 + j], ALU.mult, ALU.add, dep=[("w%d" % d, ne)])
+
+    for d in range(0, r - 1):
+        wait("v", "ld%d" % d, 16)
+        wait("a", "ld%d" % d, 16)
     wait("v", *pz)
     wait("a", *pz)
-    wait("a", *vw)
-    win = T.big[:, 0:width]
-    vs = vcn
+    win = T.big[:, 0:256 * br]
+    vs = vcv
     for k in range(kmax):
         off = T.s[:, 2 * k:2 * k + 1]
-        acf = do("a", lambda: A.activation(T.cf[:, 16 * k:16 * k + 16], win.indirect(off), ACTF.Copy, scale=T.rm[:, 0:1]), vs)
-        vs = do("v", lambda: V.tensor_scalar(T.s[:, 2 * k + 2:2 * k + 18], win.indirect(off), T.rm[:, 0:1], None, ALU.mult), vs)
-    lst = T.s[:, 2 * kmin:2 * kmin + 2 * nk]
-    m = 32 * nk
-    v1 = do("v", lambda: V.tensor_scalar(T.v1[:, 0:m], win.indirect(lst), T.n0[:, 0:1], None, ALU.mult), vs)
-    vsf = do("v", lambda: V.tensor_copy(T.sf[:, 0:kmax], T.s[:, 2:2 + 2 * kmax:2]))
-    v2 = do("v", lambda: V.tensor_tensor(T.v2[:, 0:m], T.xpb[:, 0:width].indirect(lst), T.v1[:, 0:m], ALU.add), v1, ax)
+        acf = act(T.cf[:, 16 * k:16 * k + 16], win.indirect(off), ACTF.Copy, scale=m0, dep=[vs])
+        vs = ts(T.s[:, 2 * k + 2:2 * k + 18], win.indirect(off), m0, None, ALU.mult, dep=[vs])
+    vl = ts(T.lst[:, 0:nk], T.s[:, 2 * kmin:2 * kmin + 2 * nk:2], -256 * bl, None, ALU.add, dep=[vs])
+    lst = T.lst[:, 0:nk]
+    m = 16 * nk
+    v1 = ts(T.v1[:, 0:m], T.big[:, 256 * bl:256 * br].indirect(lst), T.n0[:, 0:1], None, ALU.mult, dep=[vl])
+    vsf = cp(T.sf[:, 0:kmax], T.s[:, 2:2 + 2 * kmax:2])
+    v2 = tt(T.v2[:, 0:m], T.xpb[:, 0:256 * (br - bl)].indirect(lst), T.v1[:, 0:m], ALU.add,
+            dep=[v1, ax] + [("lx%d" % d, 16) for d in nb])
     vpx = do("v", lambda: V.tensor_tensor_scan(T.pfx[:, 1:1 + kmax], T.cf[:, 0:16 * kmax:16], T.sf[:, 0:kmax], 0.0, ALU.add, ALU.subtract),
              vsf, acf)
-    vv = T.v2[:, 0:m:32]
-    do("v", lambda: V.tensor_scalar(T.cab[:, 0:nk], vv, 4096.0, None, ALU.is_ge), v2)
-    vca = do("v", lambda: V.tensor_scalar(T.cab[:, nk:2 * nk], vv, 8192.0, None, ALU.is_ge))
-    vi = do("v", lambda: V.tensor_copy(T.vi[:, 0:nk], vv))
+    vv = T.v2[:, 0:m:16]
+    ts(T.cab[:, 0:nk], vv, 4096, None, ALU.is_ge, dep=[v2])
+    vca = ts(T.cab[:, nk:2 * nk], vv, 8192, None, ALU.is_ge)
     pp = T.pb1[:, 0:nk]
-    do("t", lambda: P.matmul(pp, T.wb[:, :], T.pfx[:, kmin:kmax + 1], True, False), vpx, vof, vcn)
-    do("t", lambda: P.matmul(pp, T.tri[:, :], T.cab[:, 0:nk], False, False), vca)
-    tp = do("t", lambda: P.matmul(pp, T.tri[:, :], T.cab[:, nk:2 * nk], False, True), vca)
-    do("v", lambda: V.tensor_scalar(T.ei[:, 0:nk], T.vi[:, 0:nk], 63, None, ALU.bitwise_and), vi)
-    v = do("v", lambda: V.tensor_scalar(T.ei[:, nk:2 * nk], T.vi[:, 0:nk], 6, 63, ALU.logical_shift_right, ALU.bitwise_and))
-    v = do("v", lambda: V.tensor_scalar(T.ef[:, 0:2 * nk], T.ei[:, 0:2 * nk], 1, None, ALU.add), v)
-    vva = do("v", lambda: V.tensor_tensor(T.val[:, 0:2 * nk], T.ef[:, 0:2 * nk], T.cab[:, 0:2 * nk], ALU.mult), v, vca)
+    mm(pp, T.wb[:, :], T.pfx[:, kmin:kmax + 1], True, False, dep=[vpx, vcn])
+    mm(pp, T.tri[:, :], T.cab[:, 0:nk], False, False, dep=[vca])
+    tp = mm(pp, T.tri[:, :], T.cab[:, nk:2 * nk], False, True)
+    ts(T.ei[:, 0:nk], vv, 63, None, ALU.bitwise_and)
+    v = ts(T.ei[:, nk:2 * nk], vv, 6, 63, ALU.logical_shift_right, ALU.bitwise_and)
+    v = ts(T.ef[:, 0:2 * nk], T.ei[:, 0:2 * nk], 1, None, ALU.add, dep=[v])
+    v = tt(T.val[:, 0:2 * nk], T.ef[:, 0:2 * nk], T.cab[:, 0:2 * nk], ALU.mult, dep=[v])
+    vgv = tt(T.gsv[:, 0:m], T.val[:, 0:2 * nk].indirect(T.gl[:, 0:nk]), T.gsr[:, 0:m], ALU.mult, dep=[v])
 
     yp = T.pb2[0:8, 0:32]
-    for x in range(2 * nk):
-        mh, kk = x // nk, x % nk
-        vo = do("v", lambda: V.tensor_scalar(T.oh[:, 32 * x:32 * x + 32], T.iot[:, 32 * mh:32 * mh + 32], T.pb1[:, kk:kk + 1],
-                                             T.val[:, x:x + 1], ALU.is_equal, ALU.mult), tp, vva, pio)
-        ty = do("t", lambda: P.matmul(yp, T.gs[:, 0:8], T.oh[:, 32 * x:32 * x + 32], x == 0, x == 2 * nk - 1), vo)
-    vy = do("v", lambda: V.tensor_scalar(T.ys[0:8, :], yp, -1.0, None, ALU.add), ty)
+    for kk in range(nk):
+        vo = ts(T.oh[:, 64 * kk:64 * kk + 64], T.iot[:, :], T.pb1[:, kk:kk + 1], None, ALU.is_equal, dep=[tp])
+        for mh in range(2):
+            x = mh * nk + kk
+            ty = mm(yp, T.gsv[:, 8 * x:8 * x + 8], T.oh[:, 64 * kk + 32 * mh:64 * kk + 32 * mh + 32], kk + mh == 0, kk + mh == nk,
+                    dep=[vo, vgv])
+    vy = ts(T.ys[0:8, :], yp, -1.0, None, ALU.add, dep=[ty])
     wait("y", *vy)
     Y.dma_start(T.y[:, :], T.ys[0:8, :]).then_inc(T.sem.yo, 16)
 

@@ -6,10 +6,10 @@ ACTF = ActivationFunctionType
 F, B, H, I4, U2 = "float32", "bfloat16", "float16", "int32", "uint16"
 SBUF = {
     I4: "syi:256 nxi:512 emi:512 ipi:8 qgi:8 v2:96 ei:16",
-    B: "syr:256 ones:128 zz:512 gcw:128 idm:128 idn:128 lwc:2048 wx:384 tri:128 wb:128 cab:16 gsv:96 oh:384",
-    H: "nxh:512 emh:512 sela:128 c1:256 cc:256 nx16:256 e16:256 pfx:32",
-    F: "ipf:8 qgf:8 mq:128 mg:128 mi:128 rm:16 rm2:16 n0:8 cu:8 bias:24 sg:128 b1:128 zw:128 i4:128 g8:96 gsr:96 l2:8 iot:64 "
-       "tri0:128 ab:4096 w0:256 w1:256 big:2048 xpb:768 cf:256 sf:16 v1:96 ef:16 val:16 ys:32",
+    B: "syr:256 ones:128 zw:128 i4:128 gcw:128 lwc:2048 wx:128 idm:128 tri:128 wb:128 cab:16 gsv:96 oh:384",
+    H: "nxh:512 emh:512 sela:128 c1:256 xe:256 xx:256 pfx:32",
+    F: "ipf:8 qgf:8 hm:8 mq:128 mg:128 mi:128 io2:256 idw:256 rm:16 rm2:16 n0:8 cu:8 bias:24 sg:128 g8:96 gsr:96 l2:8 iot:64 "
+       "tri0:128 ab:4096 w0:256 w1:256 big:2304 xpb:768 cf:256 sf:16 v1:96 ef:16 val:16 ys:32",
     U2: "uo:256 ui:2048 s:64 lst:8 gl:8",
 }
 SCRATCH = {w.split(":")[0]: ("sbuf", [128, int(w.split(":")[1])], d) for d, ws in SBUF.items() for w in ws.split()}
@@ -21,7 +21,7 @@ SCRATCH.update({
     "xdo": ("dram", [128, 16], F), "xdi": ("dram", [8, 128, 16], F),
 })
 SCRATCH.update({n: ("psum", [128, 512], F) for n in "pb0 pb1 pb2 pa0 pa1 pa2 pa3 pa4".split()})
-SEMAPHORES = ("v a t p ds dn de mo xo yo lx lw lm".split()
+SEMAPHORES = ("v a t p ds dn0 dn1 de mo xo yo lx lw lm".split()
               + [s + str(r) for s in ("x", "w", "m", "ld", "lx") for r in range(8)])
 
 
@@ -36,8 +36,6 @@ def rank_program(g, core, T, topo):
     cnt = {"v": 0, "a": 0, "t": 0, "p": 0}
     seen = {}
     nb = [d for d in (r - 1, r + 1) if 0 <= d < N]
-    bl = max(0, r - 1)
-    br = min(N, r + 2)
 
     def wait(q, name, val):
         if val > seen.get((q, name), 0):
@@ -66,139 +64,146 @@ def rank_program(g, core, T, topo):
     def act(out, in_, func, dep=(), **kw):
         return do("a", lambda: A.activation(out, in_, func, **kw), *dep)
 
-    def blk(buf, d, base=0):
-        return buf[:, 256 * (d - base):256 * (d - base) + 256]
+    def blk(buf, d):
+        return buf[:, 256 * d:256 * d + 256]
+    slot = {r: 0}
+    for d in (r + 1, r - 1):
+        if 0 <= d < N:
+            slot[d] = len(slot)
 
     for h in range(2):
         (Y, A)[h].dma_start(T.syi[0:1, 128 * h:128 * h + 128], T.sy[h::2, :]).then_inc(T.sem.ds, 16)
     for t in range(4):
-        (Y, A)[t % 2].dma_start(T.nxi[:, 128 * t:128 * t + 128], T.nx[2 * t:2 * t + 2, :]).then_inc(T.sem.dn, 16)
+        (Y, A)[t % 2].dma_start(T.nxi[:, 128 * t:128 * t + 128], T.nx[2 * t:2 * t + 2, :]).then_inc(T.sem["dn%d" % (t // 2)], 16)
     for t in range(4):
         (Y, A)[t % 2].dma_start(T.emi[:, 128 * t:128 * t + 128], T.em[2 * t:2 * t + 2, :]).then_inc(T.sem.de, 16)
-    DS, DN, DE = ("ds", 32), ("dn", 64), ("de", 64)
+    DS, DN, DE = ("ds", 32), [("dn0", 32), ("dn1", 32)], ("de", 64)
 
     def iota(ap, pattern, base, cm):
         return do("p", lambda: g.iota(ap, pattern, base, cm, allow_small_or_imprecise_dtypes=True))
     iota(T.ipi[:, 0:1], [[0, 1]], 0, 1)
     iota(T.ipf[:, 0:1], [[0, 1]], 0, 1)
     pq = iota(T.rm[:, 0:16], [[1, 16]], 0, 0)
+    pc = iota(T.mi[:, :], [[1, 128]], 0, 0)
+    pi2 = iota(T.io2[:, :], [[1, 256]], 0, 0)
     iota(T.mq[:, :], [[0, 8], [1, 16]], 0, 0)
     iota(T.mg[:, :], [[1, 8], [0, 16]], 0, 0)
-    pc = iota(T.mi[:, :], [[1, 128]], 0, 0)
     iota(T.iot[:, 0:32], [[1, 32]], 32 * r, 0)
     iota(T.iot[:, 32:64], [[1, 32]], 32 * r - 1, 0)
     iota(T.l2[:, 0:6], [[2, 6]], 0, 0)
     pio = iota(T.g8[:, :], [[0, 12], [1, 8]], 0, 0)
     for d in nb:
-        px = iota(blk(T.xpb, d, bl), [[0, 256]], 0, 0)
+        px = iota(blk(T.xpb, slot[d]), [[0, 256]], 0, 0)
     pz = px
-    if r >= 2:
-        pz = iota(T.big[:, 0:256 * bl], [[0, 256 * bl]], 0, 0)
+    if r:
+        pz = iota(T.big[:, 0:256 * r], [[0, 256 * r]], 0, 0)
 
+    BZ = 2048.0 - 4096 * 1025
     von = do("v", lambda: V.memset(T.ones[:, :], 1.0))
-    vz = do("v", lambda: V.memset(T.zz[:, :], 0.0))
     ts(T.qgi[:, 0:1], T.ipi[:, 0:1], 15, None, ALU.bitwise_and, dep=[pq])
     ts(T.qgi[:, 2:3], T.ipi[:, 0:1], 63, None, ALU.bitwise_and)
     v = ts(T.qgi[:, 1:2], T.ipi[:, 0:1], 4, None, ALU.logical_shift_right)
-    vqg = cp(T.qgf[:, 0:3], T.qgi[:, 0:3], dep=[v])
     qcol, gcol, pcol, m0 = T.qgf[:, 0:1], T.qgf[:, 1:2], T.ipf[:, 0:1], T.rm[:, 0:1]
+    ts(T.hm[:, 0:1], pcol, 64.0, None, ALU.is_lt)
+    ts(T.hm[:, 1:2], pcol, 64.0, None, ALU.is_ge)
+    vqg = cp(T.qgf[:, 0:3], T.qgi[:, 0:3], dep=[v])
     vrm = ts(T.rm[:, :], T.rm[:, :], qcol, None, ALU.is_equal, dep=[vqg])
+    v = tt(T.qgf[:, 3:4], pcol, qcol, ALU.subtract)
     ts(T.n0[:, 0:1], qcol, 0.0, None, ALU.is_gt)
     vn0 = ts(T.n0[:, 1:2], qcol, 0.0, 4096.0, ALU.is_gt, ALU.mult)
-    ts(T.sg[:, :], T.mg[:, :], gcol, None, ALU.is_equal, dep=[pc])
-    vb1 = ts(T.b1[:, :], T.mq[:, :], 0.0, 1.0 / 256, ALU.is_equal, ALU.mult)
-    ts(T.i4[:, :], T.mi[:, :], pcol, T.n0[:, 1:2], ALU.is_equal, ALU.mult, dep=[vn0])
-    vzw = tt(T.zw[:, :], T.sg[:, :], T.b1[:, :], ALU.mult, dep=[vb1])
-    vgc = tt(T.gcw[:, :], T.i4[:, :], T.zw[:, :], ALU.add, dep=[vzw])
-    cp(T.selm[0:64, :, 16:32], T.zz[0:64, 0:128], dep=[vz])
-    cp(T.selm[64:128, :, 0:16], T.zz[64:128, 0:128])
-    cp(T.tb[0:64, :, 16:32], T.zz[0:64, :])
-    cp(T.tb[64:128, :, 0:16], T.zz[64:128, :])
-
+    ts(T.zw[:, :], T.mi[:, :], T.qgf[:, 3:4], 1.0 / 256, ALU.is_equal, ALU.mult, dep=[pc, v])
     vrow = cp(T.syr[0:1, :], T.syi[0:1, :], dep=[DS])
     tbc = mm(T.pb0[:, 0:256], T.ones[0:1, :], T.syr[0:1, :], True, True, dep=[von, vrow])
-    ts(T.idm[:, :], T.mi[:, :], pcol, None, ALU.is_equal)
-    ts(T.idn[:, :], T.mi[:, :], pcol, T.n0[:, 0:1], ALU.is_equal, ALU.mult)
-    ts(T.rm2[:, :], T.rm[:, :], m0, None, ALU.max, dep=[vrm])
-    ts(T.bias[:, 0:16], T.rm[:, :], 2048.0, None, ALU.mult)
+    vi4 = ts(T.i4[:, :], T.mi[:, :], pcol, T.n0[:, 1:2], ALU.is_equal, ALU.mult, dep=[vn0])
+    vid = ts(T.idm[:, :], T.mi[:, :], pcol, None, ALU.is_equal)
+    vgc = tt(T.gcw[:, :], T.zw[:, :], T.i4[:, :], ALU.add, dep=[vi4])
+    vm0 = ts(T.n0[:, 3:4], m0, -1025.0 / 256, None, ALU.mult, dep=[vrm])
+    ts(T.rm2[:, :], T.rm[:, :], m0, None, ALU.max)
+    for h in range(2):
+        vsm = ts(T.selm[:, :, 16 * h:16 * h + 16], T.pb0[:, 128 * h:128 * h + 128], T.qgf[:, 2:3], T.hm[:, h:h + 1],
+                 ALU.is_equal, ALU.mult, dep=[tbc])
     hs = [slice(0, 64), slice(64, 128)]
     for h in range(2):
-        vsm = ts(T.selm[hs[h], :, 16 * h:16 * h + 16], T.pb0[hs[h], 128 * h:128 * h + 128], T.qgf[hs[h], 2:3], None, ALU.is_equal, dep=[tbc])
-    for h in range(2):
         vsa = ts(T.sela[hs[h], :], T.pb0[hs[h], 128 * h:128 * h + 128], T.qgf[hs[h], 2:3], None, ALU.is_equal)
-
-    def pick(out, tab, dep):
-        for seg in range(2):
-            for t in range(4):
-                x = mm(out[32 * t:32 * t + 32, 128 * seg:128 * seg + 128], T.selm[:, 2 * t + seg, :], tab[:, 128 * t:128 * t + 128],
-                       True, True, dep=dep)
-        return x
-    vnx = cp(T.nxh[:, :], T.nxi[:, :], dep=[DN])
-    txn = pick(T.pb2, T.nxh, [vsm, vnx])
-    cp(T.tb[0:64, :, 0:16], T.nxh[0:64, :], dep=[vnx])
-    vtb = cp(T.tb[64:128, :, 16:32], T.nxh[64:128, :])
-    vem = ts(T.emh[:, :], T.emi[:, :], -2048, None, ALU.add, dep=[DE])
-    txe = pick(T.pb0, T.emh, [vem, vsa])
-    for t in range(4):
-        for c in range(8):
-            tof = mm(T.pb1[32 * t:32 * t + 32, c:256:8], T.tb[:, 8 * t + c, :], T.sela[:, 32 * t:32 * t + 32], True, True, dep=[vtb, vsa])
-    v = ts(T.c1[:, :], T.pb2[:, 0:256], 1.0 / 128, 1024.502, ALU.mult, ALU.add, dep=[txn])
-    vcc = ts(T.cc[:, :], T.c1[:, :], -1025.0, None, ALU.add, dep=[v])
-    cp(T.nx16[:, 0:128], T.pb2[:, 0:128])
-    vn16 = ts(T.nx16[:, 128:256], T.pb2[:, 128:256], 128.0, None, ALU.add)
-    v = ts(T.bias[:, 16:17], m0, float(128 * (2 * r + 1)), None, ALU.mult)
-    ts(T.wx[:, 0:128], T.zw[:, :], T.rm[:, 15:16], 256.0, ALU.mult, ALU.mult)
-    vwx = ts(T.wx[:, 128:256], T.zw[:, :], T.rm[:, 15:16], -32768.0, ALU.mult, ALU.mult)
-    vbi = tt(T.bias[:, 17:18], T.bias[:, 16:17], T.bias[:, 15:16], ALU.add, dep=[v])
-    ve = cp(T.e16[:, :], T.pb0[:, 0:256], dep=[txe])
-    vxc = ts(T.wx[:, 256:384], T.mi[:, :], pcol, 4096.0, ALU.is_equal, ALU.mult)
-    ts(T.cu[:, 0:1], m0, 255.0, 1.0, ALU.mult, ALU.add)
-    ts(T.cu[:, 1:2], m0, -255.0 / 256, 1.0, ALU.mult, ALU.add)
+    act(T.bias[:, 16:17], m0, ACTF.Copy, scale=float(128 * (2 * r + 1)), dep=[vrm])
+    act(T.cu[:, 0:1], m0, ACTF.Identity, scale=255.0, bias=1.0)
+    acu = act(T.cu[:, 1:2], m0, ACTF.Identity, scale=-255.0 / 256, bias=1.0)
     for j, d in enumerate(nb):
-        vcu = ts(T.cu[:, 2 + j:3 + j], m0, float(128 * (2 * d + 1)), None, ALU.mult)
-    v = cp(T.oi[:], T.pb1[:, 0:256], dep=[tof])
-    v = ts(T.oi2[:], T.oi[:], 127, None, ALU.bitwise_and, dep=[v])
-    cp(T.off[:, :, 0:8], T.oi2[:, 0:16, :], dep=[v])
-    vof = ts(T.off[:, :, 8:16], T.oi2[:, 16:32, :], 128, None, ALU.add)
-
+        acu = act(T.cu[:, 2 + j:3 + j], m0, ACTF.Copy, scale=float(128 * (2 * d + 1)))
+    ts(T.bias[:, 0:16], T.rm[:, :], BZ, T.n0[:, 3:4], ALU.mult, ALU.add, dep=[vm0])
+    vbi = ts(T.bias[:, 17:18], m0, BZ, None, ALU.mult)
+    vxz = ts(T.xx[:, :], T.io2[:, :], 0.0, None, ALU.mult, dep=[pi2])
+    vwx = ts(T.wx[:, :], T.mi[:, :], pcol, 4096.0, ALU.is_equal, ALU.mult)
+    aid = act(T.idw[:, :], T.io2[:, :], ACTF.Identity, scale=m0, bias=T.bias[:, 16:17], dep=[acu, pi2])
     alc = {}
     for i in range(15, -1, -1):
         alc[i] = act(T.lwc[:, 128 * i:128 * i + 128], T.gcw[:, :], ACTF.Copy, scale=T.rm[:, i:i + 1], dep=[vgc])
 
-    pa = [T["pa%d" % b] for b in range(5)]
-    bank = [None] * 5
+    vn = []
+    for h in range(2):
+        vn.append(cp(T.nxh[:, 256 * h:256 * h + 256], T.nxi[:, 256 * h:256 * h + 256], dep=[DN[h]]))
+    for t in range(4):
+        for seg in range(2):
+            txn = mm(T.pb2[32 * t:32 * t + 32, 128 * seg:128 * seg + 128], T.selm[:, 2 * t + seg, :], T.nxh[:, 128 * t:128 * t + 128],
+                     True, True, dep=[vsm, vn[t // 2]])
+    vt = []
+    for u in range(2):
+        for h in range(2):
+            v = ts(T.tb[:, 16 * u:16 * u + 16, 16 * h:16 * h + 16], T.nxh[:, 256 * u:256 * u + 256], T.hm[:, h:h + 1], None, ALU.mult,
+                   dep=[vn[u]])
+        vt.append(v)
+    for t in range(4):
+        for c in range(8):
+            tof = mm(T.pb1[32 * t:32 * t + 32, c:256:8], T.tb[:, 8 * t + c, :], T.sela[:, 32 * t:32 * t + 32], True, True,
+                     dep=[vt[t // 2], vsa])
+    vc1 = ts(T.c1[:, :], T.pb2[:, 0:256], 1.0 / 128, 1024.502, ALU.mult, ALU.add, dep=[txn])
+    vem = ts(T.emh[:, :], T.emi[:, :], -2048, None, ALU.add, dep=[DE])
+    for t in range(4):
+        for seg in range(2):
+            txe = mm(T.pb0[:, 128 * seg + 32 * t:128 * seg + 32 * t + 32], T.emh[:, 128 * t:128 * t + 128], T.selm[:, 2 * t + seg, :],
+                     True, True, dep=[vem, vsa])
+    v = cp(T.oi[:], T.pb1[:, 0:256], dep=[tof])
+    v = ts(T.oi2[:], T.oi[:], 127, None, ALU.bitwise_and, dep=[v])
+    vx = cp(T.xe[:, :], T.pb0[:, 0:256], dep=[txe])
+    cp(T.off[:, :, 0:8], T.oi2[:, 0:16, :], dep=[v])
+    vx0 = ts(T.xe[:, 0:256:16], T.io2[:, 0:16], 0.0, None, ALU.mult, dep=[vx])
+    vof = ts(T.off[:, :, 8:16], T.oi2[:, 16:32, :], 128, None, ALU.add)
+    vxx = cp(T.xx[:, 0:256:16], T.pb0[:, 0:256:16], dep=[vxz])
+
+    def both(ps, w, x):
+        for b in (slice(0, 128), slice(128, 256)):
+            mm(ps[:, b], w, T.c1[:, b], True, False)
+            t = mm(ps[:, b], x[:, b], T.idm[:, :], False, True)
+        return t
     aa = {}
-    for n, i in enumerate([15, 14, 13, 12, 11, "x", 10, 9, 8, 7, 6, 5, 4, 3, 2, 1, 0]):
-        b = n % 5
-        ps = pa[b][:, 0:256]
-        deps = [vcc, ve, vn16, vwx] + ([bank[b]] if bank[b] else [])
+    wait("t", *vc1)
+    wait("t", *vid)
+    wait("t", *vx0)
+    for i in [15, 14, 13, 12, 11, 10, "x", 9, 8, 7, 6, 5, 4, 3, 2, 1, 0]:
         if i == "x":
-            ms = [(T.idm[:, :], T.e16), (T.wx[:, 256:384], T.cc)]
-            deps += [vxc]
-            o, kw = blk(T.xpb, r, bl), dict(scale=m0, bias=T.bias[:, 0:1])
+            ps = T.pa4[:, 0:256]
+            wait("t", *vwx)
+            wait("t", *vxx)
+            tm = both(ps, T.wx[:, :], T.xx)
+            o, kw = blk(T.xpb, 0), dict(scale=m0, bias=T.bias[:, 17:18])
         else:
-            ms = [(T.lwc[:, 128 * i:128 * i + 128], T.cc)]
-            deps += [alc[i]]
+            n = 15 - i
+            ps = T["pa%d" % (n % 4)][:, 0:256]
+            wait("t", *alc[i])
+            if n >= 4:
+                wait("t", *aa[i + 4])
+            tm = both(ps, T.lwc[:, 128 * i:128 * i + 128], T.xe)
             o = T.ab[:, 256 * i:256 * i + 256]
-            if i:
-                ms.append((T.idn[:, :], T.e16))
-                bc = 17 if i == 15 else i
-                kw = dict(scale=T.rm2[:, i:i + 1], bias=T.bias[:, bc:bc + 1])
-            else:
-                kw = dict(scale=m0)
-            if i == 15:
-                ms += [(T.wx[:, 0:128], T.nx16), (T.wx[:, 128:256], T.cc)]
-        for j, (lh, rh) in enumerate(ms):
-            tm = mm(ps, lh, rh[:, :], j == 0, j == len(ms) - 1, dep=deps)
-        bank[b] = aa[i] = act(o, ps, ACTF.Identity, dep=[tm, vbi], **kw)
+            kw = dict(scale=T.rm2[:, i:i + 1], bias=T.bias[:, i:i + 1]) if i else dict(scale=m0, bias=T.n0[:, 3:4])
+        aa[i] = act(o, ps, ACTF.Identity, dep=[tm, vbi], **kw)
     ax = aa["x"]
 
-    prev, vw = T.ab[:, 256 * 15:4096], aa[15]
-    for i in range(14, -1, -1):
+    prev, vw = T.idw[:, :], aid
+    for i in range(15, -1, -1):
         o = blk(T.big, r) if i == 0 else T["w%d" % (i % 2)][:, :]
         vw = tt(o, prev.indirect(T.off[:, i, :]), T.ab[:, 256 * i:256 * i + 256], ALU.add, dep=[vof, vw, aa[i]])
         prev = T["w%d" % (i % 2)][:, 0:256]
-    vu = ts(T.uo[:, :], blk(T.big, r), T.bias[:, 16:17], T.cu[:, 0:1], ALU.subtract, ALU.mult, dep=[vw, vcu])
+    vu = ts(T.uo[:, :], blk(T.big, r), T.bias[:, 16:17], T.cu[:, 0:1], ALU.subtract, ALU.mult, dep=[vw, acu])
 
     def send(buf_src, buf_dst, sem, lsem, dests):
         mask = topo.mask(core, cores[dests[0]])
@@ -210,23 +215,22 @@ def rank_program(g, core, T, topo):
                                               srcs=[buf_src], dsts=[buf_dst] * len(ids))], local_sem=T.sem[lsem])
         return len(topo.engines(core, cores[dests[0]]))
     wait("y", *ax)
-    Y.dma_start(T.xdo[:, :], blk(T.xpb, r, bl)[0:128:16, :]).then_inc(T.sem.xo, 16)
+    Y.dma_start(T.xdo[:, :], blk(T.xpb, 0)[0:128:16, :]).then_inc(T.sem.xo, 16)
     wait("p", "xo", 16)
     ne = send(T.xdo[:, :], T.xdi[r], "x%d" % r, "lx", nb)
-    far = list(range(r + 2, N))
+    far = list(range(N - 1, r, -1))
     if far:
         wait("y", *vw)
         Y.dma_start(T.mdo[:, :], blk(T.big, r)[0:128:16, :]).then_inc(T.sem.mo, 16)
-    wait("p", *vu)
-    send(T.uo[:, :], blk(T.ui, r), "w%d" % r, "lw", nb)
-    if far:
         wait("p", "mo", 16)
         send(T.mdo[:, :], T.mdi[r], "m%d" % r, "lm", far)
+    wait("p", *vu)
+    send(T.uo[:, :], blk(T.ui, r), "w%d" % r, "lw", nb)
     for d in nb:
         wait("a", *px)
         wait("a", "x%d" % d, ne)
-        A.dma_start(blk(T.xpb, d, bl)[0:128:16, :], T.xdi[d]).then_inc(T.sem["lx%d" % d], 16)
-    for d in range(0, r - 1):
+        A.dma_start(blk(T.xpb, slot[d])[0:128:16, :], T.xdi[d]).then_inc(T.sem["lx%d" % d], 16)
+    for d in range(r):
         qn = "ya"[d % 2]
         wait(qn, *pz)
         wait(qn, "m%d" % d, ne)
@@ -235,33 +239,38 @@ def rank_program(g, core, T, topo):
     kmin, kmax = max(0, 2 * r - 2), min(2 * N - 1, 2 * r + 3)
     nk = kmax - kmin + 1
     do("v", lambda: V.memset(T.s[:, :], 0))
-    cp(T.pfx[:, 0:32], T.zz[:, 0:32])
+    ts(T.pfx[:, 0:32], T.io2[:, 0:32], 0.0, None, ALU.mult)
+    vsg = ts(T.sg[:, :], T.mg[:, :], gcol, None, ALU.is_equal, dep=[pio])
     v = ts(T.tri0[:, :], T.mq[:, :], qcol, None, ALU.is_gt)
-    tt(T.tri[:, :], T.tri0[:, :], T.sg[:, :], ALU.mult, dep=[v])
+    tt(T.tri[:, :], T.tri0[:, :], T.sg[:, :], ALU.mult, dep=[v, vsg])
     ts(T.wb[:, :], T.sg[:, :], m0, 256.0, ALU.mult, ALU.mult)
     v = ts(T.n0[:, 2:3], qcol, 8.0, None, ALU.is_ge)
     ts(T.gl[:, 0:6], T.l2[:, 0:6], T.n0[:, 2:3], None, ALU.add, dep=[v, pio])
     vcn = ts(T.gsr[:, :], T.g8[:, :], gcol, None, ALU.is_equal)
-    for j, d in enumerate(nb):
-        vcv = ts(blk(T.big, d), blk(T.ui, d), T.cu[:, 1:2], T.cu[:, 2 + j:3 + j], ALU.mult, ALU.add, dep=[("w%d" % d, ne)])
 
-    for d in range(0, r - 1):
-        wait("v", "ld%d" % d, 16)
-        wait("a", "ld%d" % d, 16)
+    vs, vcv = vcn, None
     wait("v", *pz)
     wait("a", *pz)
-    win = T.big[:, 0:256 * br]
-    vs = vcv
     for k in range(kmax):
+        d = k // 2
+        if k == min(2 * r, kmax - 1):
+            for j, e in enumerate(nb):
+                vcv = ts(blk(T.big, r + slot[e]), blk(T.ui, e), T.cu[:, 1:2], T.cu[:, 2 + j:3 + j], ALU.mult, ALU.add,
+                         dep=[("w%d" % e, ne)])
+        dep = [vs] + ([("ld%d" % d, 16)] if d < r else [vw]) + ([vcv] if d > r else [])
+        win = T.big[:, 0:256 * d + 256]
         off = T.s[:, 2 * k:2 * k + 1]
-        acf = act(T.cf[:, 16 * k:16 * k + 16], win.indirect(off), ACTF.Copy, scale=m0, dep=[vs])
-        vs = ts(T.s[:, 2 * k + 2:2 * k + 18], win.indirect(off), m0, None, ALU.mult, dep=[vs])
-    vl = ts(T.lst[:, 0:nk], T.s[:, 2 * kmin:2 * kmin + 2 * nk:2], -256 * bl, None, ALU.add, dep=[vs])
+        acf = act(T.cf[:, 16 * k:16 * k + 16], win.indirect(off), ACTF.Copy, scale=m0, dep=dep)
+        vs = ts(T.s[:, 2 * k + 2:2 * k + 18], win.indirect(off), m0, None, ALU.mult, dep=dep)
+    kl = 2 if r else 0
+    if r:
+        ts(T.lst[:, 0:2], T.s[:, 2 * kmin:2 * kmin + 4:2], 256 * (slot[r - 1] - (r - 1)), None, ALU.add, dep=[vs])
+    vl = ts(T.lst[:, kl:nk], T.s[:, 2 * (kmin + kl):2 * (kmin + nk):2], -256 * r, None, ALU.add, dep=[vs])
     lst = T.lst[:, 0:nk]
     m = 16 * nk
-    v1 = ts(T.v1[:, 0:m], T.big[:, 256 * bl:256 * br].indirect(lst), T.n0[:, 0:1], None, ALU.mult, dep=[vl])
+    v1 = ts(T.v1[:, 0:m], T.big[:, 256 * r:256 * (r + len(slot))].indirect(lst), T.n0[:, 0:1], None, ALU.mult, dep=[vl, vcv])
     vsf = cp(T.sf[:, 0:kmax], T.s[:, 2:2 + 2 * kmax:2])
-    v2 = tt(T.v2[:, 0:m], T.xpb[:, 0:256 * (br - bl)].indirect(lst), T.v1[:, 0:m], ALU.add,
+    v2 = tt(T.v2[:, 0:m], T.xpb[:, 0:256 * len(slot)].indirect(lst), T.v1[:, 0:m], ALU.add,
             dep=[v1, ax] + [("lx%d" % d, 16) for d in nb])
     vpx = do("v", lambda: V.tensor_tensor_scan(T.pfx[:, 1:1 + kmax], T.cf[:, 0:16 * kmax:16], T.sf[:, 0:kmax], 0.0, ALU.add, ALU.subtract),
              vsf, acf)
@@ -274,17 +283,24 @@ def rank_program(g, core, T, topo):
     tp = mm(pp, T.tri[:, :], T.cab[:, nk:2 * nk], False, True)
     ts(T.ei[:, 0:nk], vv, 63, None, ALU.bitwise_and)
     v = ts(T.ei[:, nk:2 * nk], vv, 6, 63, ALU.logical_shift_right, ALU.bitwise_and)
-    v = ts(T.ef[:, 0:2 * nk], T.ei[:, 0:2 * nk], 1, None, ALU.add, dep=[v])
-    v = tt(T.val[:, 0:2 * nk], T.ef[:, 0:2 * nk], T.cab[:, 0:2 * nk], ALU.mult, dep=[v])
-    vgv = tt(T.gsv[:, 0:m], T.val[:, 0:2 * nk].indirect(T.gl[:, 0:nk]), T.gsr[:, 0:m], ALU.mult, dep=[v])
 
+    vo = {}
+
+    def onehot(kk):
+        vo[kk] = ts(T.oh[:, 64 * kk:64 * kk + 64], T.iot[:, :], T.pb1[:, kk:kk + 1], None, ALU.is_equal, dep=[tp])
+    v = ts(T.ef[:, 0:2 * nk], T.ei[:, 0:2 * nk], 1, None, ALU.add, dep=[v])
+    onehot(0)
+    v = tt(T.val[:, 0:2 * nk], T.ef[:, 0:2 * nk], T.cab[:, 0:2 * nk], ALU.mult, dep=[v])
+    onehot(1)
+    vgv = tt(T.gsv[:, 0:m], T.val[:, 0:2 * nk].indirect(T.gl[:, 0:nk]), T.gsr[:, 0:m], ALU.mult, dep=[v])
     yp = T.pb2[0:8, 0:32]
     for kk in range(nk):
-        vo = ts(T.oh[:, 64 * kk:64 * kk + 64], T.iot[:, :], T.pb1[:, kk:kk + 1], None, ALU.is_equal, dep=[tp])
+        if kk > 1:
+            onehot(kk)
         for mh in range(2):
             x = mh * nk + kk
             ty = mm(yp, T.gsv[:, 8 * x:8 * x + 8], T.oh[:, 64 * kk + 32 * mh:64 * kk + 32 * mh + 32], kk + mh == 0, kk + mh == nk,
-                    dep=[vo, vgv])
+                    dep=[vo[kk], vgv])
     vy = ts(T.ys[0:8, :], yp, -1.0, None, ALU.add, dep=[ty])
     wait("y", *vy)
     Y.dma_start(T.y[:, :], T.ys[0:8, :]).then_inc(T.sem.yo, 16)

@@ -5,24 +5,26 @@ ALU = AluOpType
 ACTF = ActivationFunctionType
 F, B, H, I4, U2 = "float32", "bfloat16", "float16", "int32", "uint16"
 SBUF = {
-    I4: "syi:256 nxi:512 emi:512 ipi:8 qgi:8 v2:96 ei:16",
-    B: "syr:256 ones:128 zw:128 i4:128 gcw:128 lwc:2048 wx:128 idm:128 tri:128 wb:128 cab:16 gsv:96 oh:384",
-    H: "nxh:512 emh:512 sela:128 c1:256 xe:256 xx:256 pfx:32",
-    F: "ipf:8 qgf:8 hm:8 mq:128 mg:128 mi:128 io2:256 idw:256 rm:16 rm2:16 n0:8 cu:8 bias:24 sg:128 g8:96 gsr:96 l2:8 iot:64 "
-       "tri0:128 ab:4096 w0:256 w1:256 big:2304 xpb:768 cf:256 sf:16 v1:96 ef:16 val:16 ys:32",
-    U2: "uo:256 ui:2048 s:64 lst:8 gl:8",
+    I4: "nxi:512 emi:512 ipi:8 qgi:8 v2:96 ei:16",
+    B: "syr:256 ones:128 zw:128 zw0:128 wx:128 c1:256 cc:256 tri:128 wb:128 cab:16 gsv:96 oh:384",
+    H: "nxh:512 emh:512 sela:128 pfx:32",
+    F: "ipf:8 qgf:8 hm:8 mq:128 mg:128 mi:128 io2:256 idw:256 rm:16 n0:8 cu:8 bias:24 sg:128 g8:96 gsr:96 l2:8 iot:64 "
+       "tri0:128 ab:4096 w0:256 w1:256 big:2304 cnt:2304 xpb:256 pay:768 cf:256 ef:16 val:16 ys:32",
+    U2: "uo:256 ui:2048 s:64 lst:8 lsc:24 gl:8",
 }
 SCRATCH = {w.split(":")[0]: ("sbuf", [128, int(w.split(":")[1])], d) for d, ws in SBUF.items() for w in ws.split()}
 SCRATCH.update({
+    "syi": ("sbuf", [128, 8, 32], I4),
     "selm": ("sbuf", [128, 8, 32], H), "tb": ("sbuf", [128, 32, 32], H),
-    "oi": ("sbuf", [128, 32, 8], I4), "oi2": ("sbuf", [128, 32, 8], I4),
+    "oi": ("sbuf", [128, 16, 16], I4), "oi2": ("sbuf", [128, 16, 16], I4),
     "off": ("sbuf", [128, 16, 16], U2),
     "mdo": ("dram", [128, 16], F), "mdi": ("dram", [8, 128, 16], F),
+    "cdo": ("dram", [128, 16], F), "cdi": ("dram", [8, 128, 16], F),
     "xdo": ("dram", [128, 16], F), "xdi": ("dram", [8, 128, 16], F),
 })
-SCRATCH.update({n: ("psum", [128, 512], F) for n in "pb0 pb1 pb2 pa0 pa1 pa2 pa3 pa4".split()})
-SEMAPHORES = ("v a t p ds dn0 dn1 de mo xo yo lx lw lm".split()
-              + [s + str(r) for s in ("x", "w", "m", "ld", "lx") for r in range(8)])
+SCRATCH.update({n: ("psum", [128, 512], F) for n in "pb0 pb1 pb2 pa0 pa1 pa2".split()})
+SEMAPHORES = ("v a t p ds dn0 dn1 de mo xo co yo lx lw lm lc".split()
+              + [s + str(r) for s in ("x", "w", "m", "c", "ld", "lx", "lc") for r in range(8)])
 
 
 def rank_program(g, core, T, topo):
@@ -35,7 +37,7 @@ def rank_program(g, core, T, topo):
     eng = {"v": V, "a": A, "t": P, "p": g, "y": Y}
     cnt = {"v": 0, "a": 0, "t": 0, "p": 0}
     seen = {}
-    nb = [d for d in (r - 1, r + 1) if 0 <= d < N]
+    nb = [d for d in (r + 1, r - 1) if 0 <= d < N]
 
     def wait(q, name, val):
         if val > seen.get((q, name), 0):
@@ -66,13 +68,13 @@ def rank_program(g, core, T, topo):
 
     def blk(buf, d):
         return buf[:, 256 * d:256 * d + 256]
+    hf = [slice(0, 128), slice(128, 256)]
     slot = {r: 0}
-    for d in (r + 1, r - 1):
-        if 0 <= d < N:
-            slot[d] = len(slot)
+    for d in nb:
+        slot[d] = len(slot)
 
     for h in range(2):
-        (Y, A)[h].dma_start(T.syi[0:1, 128 * h:128 * h + 128], T.sy[h::2, :]).then_inc(T.sem.ds, 16)
+        (Y, A)[h].dma_start(T.syi[0:1, 4 * h:4 * h + 4, :], T.sy[h::2, :]).then_inc(T.sem.ds, 16)
     for t in range(4):
         (Y, A)[t % 2].dma_start(T.nxi[:, 128 * t:128 * t + 128], T.nx[2 * t:2 * t + 2, :]).then_inc(T.sem["dn%d" % (t // 2)], 16)
     for t in range(4):
@@ -92,13 +94,14 @@ def rank_program(g, core, T, topo):
     iota(T.iot[:, 32:64], [[1, 32]], 32 * r - 1, 0)
     iota(T.l2[:, 0:6], [[2, 6]], 0, 0)
     pio = iota(T.g8[:, :], [[0, 12], [1, 8]], 0, 0)
-    for d in nb:
-        px = iota(blk(T.xpb, slot[d]), [[0, 256]], 0, 0)
-    pz = px
+    pz = pio
     if r:
         pz = iota(T.big[:, 0:256 * r], [[0, 256 * r]], 0, 0)
+    zeros = 256 * min(N, r + 2)
+    pcz = iota(T.cnt[:, 0:zeros], [[0, zeros]], 0, 0)
 
-    BZ = 2048.0 - 4096 * 1025
+    CB = 129
+    BZ = 2047.0 - 4096 * CB
     von = do("v", lambda: V.memset(T.ones[:, :], 1.0))
     ts(T.qgi[:, 0:1], T.ipi[:, 0:1], 15, None, ALU.bitwise_and, dep=[pq])
     ts(T.qgi[:, 2:3], T.ipi[:, 0:1], 63, None, ALU.bitwise_and)
@@ -108,102 +111,103 @@ def rank_program(g, core, T, topo):
     ts(T.hm[:, 1:2], pcol, 64.0, None, ALU.is_ge)
     vqg = cp(T.qgf[:, 0:3], T.qgi[:, 0:3], dep=[v])
     vrm = ts(T.rm[:, :], T.rm[:, :], qcol, None, ALU.is_equal, dep=[vqg])
-    v = tt(T.qgf[:, 3:4], pcol, qcol, ALU.subtract)
-    ts(T.n0[:, 0:1], qcol, 0.0, None, ALU.is_gt)
-    vn0 = ts(T.n0[:, 1:2], qcol, 0.0, 4096.0, ALU.is_gt, ALU.mult)
-    ts(T.zw[:, :], T.mi[:, :], T.qgf[:, 3:4], 1.0 / 256, ALU.is_equal, ALU.mult, dep=[pc, v])
-    vrow = cp(T.syr[0:1, :], T.syi[0:1, :], dep=[DS])
+    vg16 = tt(T.qgf[:, 3:4], pcol, qcol, ALU.subtract)
+    vbi = ts(T.bias[:, 0:16], T.rm[:, :], BZ, None, ALU.mult, dep=[vrm])
+    vwx = ts(T.wx[:, :], T.mi[:, :], pcol, 4096.0, ALU.is_equal, ALU.mult, dep=[pc])
+    v = ts(T.zw[:, :], T.mi[:, :], T.qgf[:, 3:4], 1.0 / 256, ALU.is_equal, ALU.mult, dep=[vg16])
+    vzw = ts(T.zw0[:, :], T.zw[:, :], m0, None, ALU.mult, dep=[v])
+    for seg in range(2):
+        mm(T["pa%d" % seg][:, 0:128], T.ones[0:1, :], T.ones[0:1, :], True, False, dep=[von])
+    for seg in range(2):
+        vrow = cp(T.syr[0:1, seg:256:2], T.syi[0:1, :, 16 * seg:16 * seg + 16], dep=[DS])
     tbc = mm(T.pb0[:, 0:256], T.ones[0:1, :], T.syr[0:1, :], True, True, dep=[von, vrow])
-    vi4 = ts(T.i4[:, :], T.mi[:, :], pcol, T.n0[:, 1:2], ALU.is_equal, ALU.mult, dep=[vn0])
-    vid = ts(T.idm[:, :], T.mi[:, :], pcol, None, ALU.is_equal)
-    vgc = tt(T.gcw[:, :], T.zw[:, :], T.i4[:, :], ALU.add, dep=[vi4])
-    vm0 = ts(T.n0[:, 3:4], m0, -1025.0 / 256, None, ALU.mult, dep=[vrm])
-    ts(T.rm2[:, :], T.rm[:, :], m0, None, ALU.max)
+    act(T.bias[:, 16:17], m0, ACTF.Copy, scale=float(128 * (2 * r + 1)), dep=[vrm])
+    act(T.bias[:, 18:19], m0, ACTF.Copy, scale=-17 * CB / 256.0)
+    act(T.cu[:, 0:1], m0, ACTF.Identity, scale=255.0, bias=1.0)
+    act(T.cu[:, 1:2], m0, ACTF.Identity, scale=-255.0 / 256, bias=1.0)
+    acu = act(T.cu[:, 2:3], m0, ACTF.Copy, scale=float(128 * (2 * r + 3)))
+    aid = act(T.idw[:, :], T.io2[:, :], ACTF.Identity, scale=m0, bias=T.bias[:, 16:17], dep=[acu, pi2])
+
+    def cast(h):
+        return cp(T.nxh[:, 256 * h:256 * h + 256], T.nxi[:, 256 * h:256 * h + 256], dep=[DN[h]])
+    vn = [cast(0)]
     for h in range(2):
-        vsm = ts(T.selm[:, :, 16 * h:16 * h + 16], T.pb0[:, 128 * h:128 * h + 128], T.qgf[:, 2:3], T.hm[:, h:h + 1],
-                 ALU.is_equal, ALU.mult, dep=[tbc])
+        for seg in range(2):
+            vsm = ts(T.selm[:, seg:8:2, 16 * h:16 * h + 16], T.pb0[:, 128 * h + seg:128 * h + 128:2], T.qgf[:, 2:3], T.hm[:, h:h + 1],
+                     ALU.is_equal, ALU.mult, dep=[tbc])
+    vn.append(cast(1))
     hs = [slice(0, 64), slice(64, 128)]
     for h in range(2):
         vsa = ts(T.sela[hs[h], :], T.pb0[hs[h], 128 * h:128 * h + 128], T.qgf[hs[h], 2:3], None, ALU.is_equal)
-    act(T.bias[:, 16:17], m0, ACTF.Copy, scale=float(128 * (2 * r + 1)), dep=[vrm])
-    act(T.cu[:, 0:1], m0, ACTF.Identity, scale=255.0, bias=1.0)
-    acu = act(T.cu[:, 1:2], m0, ACTF.Identity, scale=-255.0 / 256, bias=1.0)
-    for j, d in enumerate(nb):
-        acu = act(T.cu[:, 2 + j:3 + j], m0, ACTF.Copy, scale=float(128 * (2 * d + 1)))
-    ts(T.bias[:, 0:16], T.rm[:, :], BZ, T.n0[:, 3:4], ALU.mult, ALU.add, dep=[vm0])
-    vbi = ts(T.bias[:, 17:18], m0, BZ, None, ALU.mult)
-    vxz = ts(T.xx[:, :], T.io2[:, :], 0.0, None, ALU.mult, dep=[pi2])
-    vwx = ts(T.wx[:, :], T.mi[:, :], pcol, 4096.0, ALU.is_equal, ALU.mult)
-    aid = act(T.idw[:, :], T.io2[:, :], ACTF.Identity, scale=m0, bias=T.bias[:, 16:17], dep=[acu, pi2])
-    alc = {}
-    for i in range(15, -1, -1):
-        alc[i] = act(T.lwc[:, 128 * i:128 * i + 128], T.gcw[:, :], ACTF.Copy, scale=T.rm[:, i:i + 1], dep=[vgc])
-
-    vn = []
-    for h in range(2):
-        vn.append(cp(T.nxh[:, 256 * h:256 * h + 256], T.nxi[:, 256 * h:256 * h + 256], dep=[DN[h]]))
-    for t in range(4):
-        for seg in range(2):
-            txn = mm(T.pb2[32 * t:32 * t + 32, 128 * seg:128 * seg + 128], T.selm[:, 2 * t + seg, :], T.nxh[:, 128 * t:128 * t + 128],
-                     True, True, dep=[vsm, vn[t // 2]])
     vt = []
     for u in range(2):
         for h in range(2):
             v = ts(T.tb[:, 16 * u:16 * u + 16, 16 * h:16 * h + 16], T.nxh[:, 256 * u:256 * u + 256], T.hm[:, h:h + 1], None, ALU.mult,
                    dep=[vn[u]])
         vt.append(v)
+    vem = ts(T.emh[:, :], T.emi[:, :], -2048, None, ALU.add, dep=[DE])
+
+    for t in range(4):
+        for seg in range(2):
+            txn = mm(T.pb2[32 * t:32 * t + 32, hf[seg]], T.selm[:, 2 * t + seg, :], T.nxh[:, 128 * t:128 * t + 128],
+                     True, True, dep=[vsm, vn[t // 2]])
     for t in range(4):
         for c in range(8):
             tof = mm(T.pb1[32 * t:32 * t + 32, c:256:8], T.tb[:, 8 * t + c, :], T.sela[:, 32 * t:32 * t + 32], True, True,
                      dep=[vt[t // 2], vsa])
-    vc1 = ts(T.c1[:, :], T.pb2[:, 0:256], 1.0 / 128, 1024.502, ALU.mult, ALU.add, dep=[txn])
-    vem = ts(T.emh[:, :], T.emi[:, :], -2048, None, ALU.add, dep=[DE])
-    for t in range(4):
-        for seg in range(2):
-            txe = mm(T.pb0[:, 128 * seg + 32 * t:128 * seg + 32 * t + 32], T.emh[:, 128 * t:128 * t + 128], T.selm[:, 2 * t + seg, :],
-                     True, True, dep=[vem, vsa])
-    v = cp(T.oi[:], T.pb1[:, 0:256], dep=[tof])
-    v = ts(T.oi2[:], T.oi[:], 127, None, ALU.bitwise_and, dep=[v])
-    vx = cp(T.xe[:, :], T.pb0[:, 0:256], dep=[txe])
-    cp(T.off[:, :, 0:8], T.oi2[:, 0:16, :], dep=[v])
-    vx0 = ts(T.xe[:, 0:256:16], T.io2[:, 0:16], 0.0, None, ALU.mult, dep=[vx])
-    vof = ts(T.off[:, :, 8:16], T.oi2[:, 16:32, :], 128, None, ALU.add)
-    vxx = cp(T.xx[:, 0:256:16], T.pb0[:, 0:256:16], dep=[vxz])
-
-    def both(ps, w, x):
-        for b in (slice(0, 128), slice(128, 256)):
-            mm(ps[:, b], w, T.c1[:, b], True, False)
-            t = mm(ps[:, b], x[:, b], T.idm[:, :], False, True)
-        return t
+    ac1 = act(T.c1[:, :], T.pb2[:, 0:256], ACTF.Copy, scale=1.0 / 128, bias=CB - 0.498, dep=[txn])
+    tpx = []
+    for seg in range(2):
+        for t in range(4):
+            mm(T["pa%d" % seg][32 * t:32 * t + 32, 0:128], T.selm[:, 2 * t + seg, :], T.emh[:, 128 * t:128 * t + 128], False, False,
+               dep=[vem])
+        tpx.append(mm(T["pa%d" % seg][:, 0:128], T.wx[:, :], T.c1[:, hf[seg]], False, True, dep=[vwx, ac1]))
     aa = {}
-    wait("t", *vc1)
-    wait("t", *vid)
-    wait("t", *vx0)
-    for i in [15, 14, 13, 12, 11, 10, "x", 9, 8, 7, 6, 5, 4, 3, 2, 1, 0]:
-        if i == "x":
-            ps = T.pa4[:, 0:256]
-            wait("t", *vwx)
-            wait("t", *vxx)
-            tm = both(ps, T.wx[:, :], T.xx)
-            o, kw = blk(T.xpb, 0), dict(scale=m0, bias=T.bias[:, 17:18])
+    for i in [15, 14, 13, 0, 12, 11, 10, 9, 8, 7, 6, 5, 4, 3, 2, 1]:
+        for seg in range(2):
+            o = T.ab[:, 256 * i + 128 * seg:256 * i + 128 * seg + 128] if i else T.xpb[:, hf[seg]]
+            aa[i, seg] = act(o, T["pa%d" % seg][:, 0:128], ACTF.Identity, dep=[tpx[seg], vbi], scale=T.rm[:, i:i + 1],
+                             bias=T.bias[:, i:i + 1])
+    ax = aa[0, 1]
+
+    vof = {}
+
+    def lists(lo, hi, part):
+        a, b = 16 * lo, 16 * hi
+        if part == 0:
+            vof["x"] = cp(T.oi[:, lo:hi, :], T.pb1[:, a:b], dep=[tof])
+        elif part == 1:
+            vof["x"] = ts(T.oi2[:, lo:hi, :], T.oi[:, lo:hi, :], 127, None, ALU.bitwise_and, dep=[vof["x"]])
         else:
-            n = 15 - i
-            ps = T["pa%d" % (n % 4)][:, 0:256]
-            wait("t", *alc[i])
-            if n >= 4:
-                wait("t", *aa[i + 4])
-            tm = both(ps, T.lwc[:, 128 * i:128 * i + 128], T.xe)
-            o = T.ab[:, 256 * i:256 * i + 256]
-            kw = dict(scale=T.rm2[:, i:i + 1], bias=T.bias[:, i:i + 1]) if i else dict(scale=m0, bias=T.n0[:, 3:4])
-        aa[i] = act(o, ps, ACTF.Identity, dep=[tm, vbi], **kw)
-    ax = aa["x"]
+            cp(T.off[:, lo:hi, 0:8], T.oi2[:, lo:hi, 0:8], dep=[vof["x"]])
+            x = ts(T.off[:, lo:hi, 8:16], T.oi2[:, lo:hi, 8:16], 128, None, ALU.add)
+            for i in range(lo, hi):
+                vof[i] = x
+    todo = [(lo, hi, part) for lo, hi in [(12, 16), (8, 12), (0, 8)] for part in range(3)]
+    for _ in range(3):
+        lists(*todo.pop(0))
 
     prev, vw = T.idw[:, :], aid
     for i in range(15, -1, -1):
-        o = blk(T.big, r) if i == 0 else T["w%d" % (i % 2)][:, :]
-        vw = tt(o, prev.indirect(T.off[:, i, :]), T.ab[:, 256 * i:256 * i + 256], ALU.add, dep=[vof, vw, aa[i]])
-        prev = T["w%d" % (i % 2)][:, 0:256]
+        o = T["w%d" % (i % 2)][:, :] if i else blk(T.big, r)
+        if i == 15:
+            for seg in range(2):
+                vw = tt(o[:, hf[seg]], prev.indirect(T.off[:, i, 8 * seg:8 * seg + 8]),
+                        T.ab[:, 256 * i + 128 * seg:256 * i + 128 * seg + 128], ALU.add, dep=[vof[i], aid, aa[i, seg]])
+        elif i:
+            vw = tt(o, prev.indirect(T.off[:, i, :]), T.ab[:, 256 * i:256 * i + 256], ALU.add, dep=[vof[i], vw, aa[i, 1]])
+        else:
+            vw = cp(o, prev.indirect(T.off[:, i, :]), dep=[vof[i], vw])
+        prev = o
+        if todo:
+            lists(*todo.pop(0))
     vu = ts(T.uo[:, :], blk(T.big, r), T.bias[:, 16:17], T.cu[:, 0:1], ALU.subtract, ALU.mult, dep=[vw, acu])
+    pcn = T.pa2[:, 0:256]
+    mm(pcn, T.zw0[:, :], T.c1[:, :], True, False, dep=[vzw])
+    acc = act(T.cc[:, :], blk(T.big, r), ACTF.Copy, scale=1.0 / 4096, bias=CB - 0.5 + 1.0 / 8192, dep=[vw])
+    tcn = mm(pcn, T.zw[:, :], T.cc[:, :], False, True, dep=[acc])
+    acn = act(blk(T.cnt, r), pcn, ACTF.Identity, bias=T.bias[:, 18:19], dep=[tcn, pcz, acu])
+    apy = act(blk(T.pay, 0), blk(T.big, r), ACTF.Copy)
 
     def send(buf_src, buf_dst, sem, lsem, dests):
         mask = topo.mask(core, cores[dests[0]])
@@ -215,21 +219,24 @@ def rank_program(g, core, T, topo):
                                               srcs=[buf_src], dsts=[buf_dst] * len(ids))], local_sem=T.sem[lsem])
         return len(topo.engines(core, cores[dests[0]]))
     wait("y", *ax)
-    Y.dma_start(T.xdo[:, :], blk(T.xpb, 0)[0:128:16, :]).then_inc(T.sem.xo, 16)
+    Y.dma_start(T.xdo[:, :], T.xpb[0:128:16, :]).then_inc(T.sem.xo, 16)
     wait("p", "xo", 16)
     ne = send(T.xdo[:, :], T.xdi[r], "x%d" % r, "lx", nb)
+    wait("p", *vu)
+    send(T.uo[:, :], blk(T.ui, r), "w%d" % r, "lw", nb)
     far = list(range(N - 1, r, -1))
     if far:
         wait("y", *vw)
         Y.dma_start(T.mdo[:, :], blk(T.big, r)[0:128:16, :]).then_inc(T.sem.mo, 16)
         wait("p", "mo", 16)
         send(T.mdo[:, :], T.mdi[r], "m%d" % r, "lm", far)
-    wait("p", *vu)
-    send(T.uo[:, :], blk(T.ui, r), "w%d" % r, "lw", nb)
-    for d in nb:
-        wait("a", *px)
-        wait("a", "x%d" % d, ne)
-        A.dma_start(blk(T.xpb, slot[d])[0:128:16, :], T.xdi[d]).then_inc(T.sem["lx%d" % d], 16)
+    wait("y", *acn)
+    Y.dma_start(T.cdo[:, :], blk(T.cnt, r)[0:128:16, :]).then_inc(T.sem.co, 16)
+    wait("p", "co", 16)
+    send(T.cdo[:, :], T.cdi[r], "c%d" % r, "lc", far + ([r - 1] if r else []))
+    wait("a", "xo", 16)
+    wait("a", *apy)
+    A.dma_start(blk(T.pay, 0)[0:128:16, :], T.xdo[:, :]).then_inc(T.sem["lx%d" % r], 16)
     for d in range(r):
         qn = "ya"[d % 2]
         wait(qn, *pz)
@@ -248,55 +255,64 @@ def rank_program(g, core, T, topo):
     ts(T.gl[:, 0:6], T.l2[:, 0:6], T.n0[:, 2:3], None, ALU.add, dep=[v, pio])
     vcn = ts(T.gsr[:, :], T.g8[:, :], gcol, None, ALU.is_equal)
 
-    vs, vcv = vcn, None
+    for e in nb:
+        wait("y", "x%d" % e, ne)
+        wait("y", *cp(blk(T.pay, slot[e]), blk(T.ui, e), dep=[("w%d" % e, ne)]))
+        Y.dma_start(blk(T.pay, slot[e])[0:128:16, :], T.xdi[e]).then_inc(T.sem["lx%d" % e], 16)
+        if e > r:
+            vcv = ts(blk(T.big, e), blk(T.ui, e), T.cu[:, 1:2], T.cu[:, 2:3], ALU.mult, ALU.add, dep=[acu])
+    cin = [d for d in range(min(N, r + 2)) if d != r]
+    for d in cin:
+        wait("y", *pcz)
+        wait("y", "c%d" % d, ne)
+        Y.dma_start(blk(T.cnt, d)[0:128:16, :], T.cdi[d]).then_inc(T.sem["lc%d" % d], 16)
+
+    vs = vcn
     wait("v", *pz)
-    wait("a", *pz)
-    for k in range(kmax):
+    ka = max(0, kmax - 5)
+    for k in range(kmax + 1):
+        if k in (ka, kmax) and k:
+            a = 0 if k == ka else ka
+            b = a + a % 2
+            v = cp(T.lsc[:, b:b + k - a], T.s[:, 2 * a:2 * k:2], dep=[vs])
+            acf = act(T.cf[:, 16 * a:16 * k], T.cnt[:, 0:zeros].indirect(T.lsc[:, b:b + k - a]), ACTF.Copy, scale=m0,
+                      dep=[v, acn, pcz] + [("lc%d" % d, 16) for d in cin])
+        if k == kmax:
+            break
         d = k // 2
-        if k == min(2 * r, kmax - 1):
-            for j, e in enumerate(nb):
-                vcv = ts(blk(T.big, r + slot[e]), blk(T.ui, e), T.cu[:, 1:2], T.cu[:, 2 + j:3 + j], ALU.mult, ALU.add,
-                         dep=[("w%d" % e, ne)])
-        dep = [vs] + ([("ld%d" % d, 16)] if d < r else [vw]) + ([vcv] if d > r else [])
         win = T.big[:, 0:256 * d + 256]
         off = T.s[:, 2 * k:2 * k + 1]
-        acf = act(T.cf[:, 16 * k:16 * k + 16], win.indirect(off), ACTF.Copy, scale=m0, dep=dep)
-        vs = ts(T.s[:, 2 * k + 2:2 * k + 18], win.indirect(off), m0, None, ALU.mult, dep=dep)
+        vs = ts(T.s[:, 2 * k + 2:2 * k + 18], win.indirect(off), m0, None, ALU.mult,
+                dep=[vs] + ([("ld%d" % d, 16)] if d < r else [vw]) + ([vcv] if d > r else []))
     kl = 2 if r else 0
     if r:
         ts(T.lst[:, 0:2], T.s[:, 2 * kmin:2 * kmin + 4:2], 256 * (slot[r - 1] - (r - 1)), None, ALU.add, dep=[vs])
     vl = ts(T.lst[:, kl:nk], T.s[:, 2 * (kmin + kl):2 * (kmin + nk):2], -256 * r, None, ALU.add, dep=[vs])
     lst = T.lst[:, 0:nk]
     m = 16 * nk
-    v1 = ts(T.v1[:, 0:m], T.big[:, 256 * r:256 * (r + len(slot))].indirect(lst), T.n0[:, 0:1], None, ALU.mult, dep=[vl, vcv])
-    vsf = cp(T.sf[:, 0:kmax], T.s[:, 2:2 + 2 * kmax:2])
-    v2 = tt(T.v2[:, 0:m], T.xpb[:, 0:256 * len(slot)].indirect(lst), T.v1[:, 0:m], ALU.add,
-            dep=[v1, ax] + [("lx%d" % d, 16) for d in nb])
-    vpx = do("v", lambda: V.tensor_tensor_scan(T.pfx[:, 1:1 + kmax], T.cf[:, 0:16 * kmax:16], T.sf[:, 0:kmax], 0.0, ALU.add, ALU.subtract),
-             vsf, acf)
+    v2 = cp(T.v2[:, 0:m], T.pay[:, 0:256 * len(slot)].indirect(lst), dep=[vl] + [("lx%d" % d, 16) for d in slot])
     vv = T.v2[:, 0:m:16]
     ts(T.cab[:, 0:nk], vv, 4096, None, ALU.is_ge, dep=[v2])
     vca = ts(T.cab[:, nk:2 * nk], vv, 8192, None, ALU.is_ge)
-    pp = T.pb1[:, 0:nk]
-    mm(pp, T.wb[:, :], T.pfx[:, kmin:kmax + 1], True, False, dep=[vpx, vcn])
-    mm(pp, T.tri[:, :], T.cab[:, 0:nk], False, False, dep=[vca])
-    tp = mm(pp, T.tri[:, :], T.cab[:, nk:2 * nk], False, True)
     ts(T.ei[:, 0:nk], vv, 63, None, ALU.bitwise_and)
-    v = ts(T.ei[:, nk:2 * nk], vv, 6, 63, ALU.logical_shift_right, ALU.bitwise_and)
+    ve = ts(T.ei[:, nk:2 * nk], vv, 6, 63, ALU.logical_shift_right, ALU.bitwise_and)
+    vpx = do("v", lambda: V.tensor_tensor_scan(T.pfx[:, 1:1 + kmax], T.cf[:, 0:16 * kmax:16], T.cf[:, 0:16 * kmax:16], 0.0, ALU.add, ALU.max),
+             acf)
+    pp = T.pb1[:, 0:nk]
+    mm(pp, T.tri[:, :], T.cab[:, 0:nk], True, False, dep=[vca, vcn])
+    mm(pp, T.tri[:, :], T.cab[:, nk:2 * nk], False, False)
+    tp = mm(pp, T.wb[:, :], T.pfx[:, kmin:kmax + 1], False, True, dep=[vpx])
 
     vo = {}
 
     def onehot(kk):
         vo[kk] = ts(T.oh[:, 64 * kk:64 * kk + 64], T.iot[:, :], T.pb1[:, kk:kk + 1], None, ALU.is_equal, dep=[tp])
-    v = ts(T.ef[:, 0:2 * nk], T.ei[:, 0:2 * nk], 1, None, ALU.add, dep=[v])
-    onehot(0)
+    v = ts(T.ef[:, 0:2 * nk], T.ei[:, 0:2 * nk], 1, None, ALU.add, dep=[ve])
     v = tt(T.val[:, 0:2 * nk], T.ef[:, 0:2 * nk], T.cab[:, 0:2 * nk], ALU.mult, dep=[v])
-    onehot(1)
     vgv = tt(T.gsv[:, 0:m], T.val[:, 0:2 * nk].indirect(T.gl[:, 0:nk]), T.gsr[:, 0:m], ALU.mult, dep=[v])
     yp = T.pb2[0:8, 0:32]
     for kk in range(nk):
-        if kk > 1:
-            onehot(kk)
+        onehot(kk)
         for mh in range(2):
             x = mh * nk + kk
             ty = mm(yp, T.gsv[:, 8 * x:8 * x + 8], T.oh[:, 64 * kk + 32 * mh:64 * kk + 32 * mh + 32], kk + mh == 0, kk + mh == nk,
@@ -308,6 +324,7 @@ def rank_program(g, core, T, topo):
     wait("y", "yo", 16)
     wait("p", "lx", ne)
     wait("p", "lw", ne)
+    wait("p", "lc", ne)
     if far:
         wait("p", "lm", ne)
     for name in ("v", "a", "t"):

from concourse.bass import DstId, RemoteDMATransfer
from concourse.mybir import AluOpType, ActivationFunctionType

ALU = AluOpType
ACTF = ActivationFunctionType
F, B, H, I4, U2 = "float32", "bfloat16", "float16", "int32", "uint16"
SBUF = {
    I4: "nxi:512 emi:512 ipi:8 qgi:8 v2:96 ei:16",
    B: "syr:256 ones:128 zw:128 zw0:128 wx:128 c1:256 cc:256 tri:128 wb:128 cab:16 gsv:96 oh:384",
    H: "nxh:512 emh:512 sela:128 pfx:32",
    F: "ipf:8 qgf:8 hm:8 mq:128 mg:128 mi:128 io2:256 idw:256 rm:16 n0:8 cu:8 bias:24 sg:128 g8:96 gsr:96 l2:8 iot:64 "
       "tri0:128 ab:4096 w0:256 w1:256 big:2304 cnt:2304 xpb:256 pay:768 cf:256 ef:16 val:16 ys:32",
    U2: "uo:256 ui:2048 s:64 lst:8 lsc:24 gl:8",
}
SCRATCH = {w.split(":")[0]: ("sbuf", [128, int(w.split(":")[1])], d) for d, ws in SBUF.items() for w in ws.split()}
SCRATCH.update({
    "syi": ("sbuf", [128, 8, 32], I4),
    "selm": ("sbuf", [128, 8, 32], H), "tb": ("sbuf", [128, 32, 32], H),
    "oi": ("sbuf", [128, 16, 16], I4), "oi2": ("sbuf", [128, 16, 16], I4),
    "off": ("sbuf", [128, 16, 16], U2),
    "mdo": ("dram", [128, 16], F), "mdi": ("dram", [8, 128, 16], F),
    "cdo": ("dram", [128, 16], F), "cdi": ("dram", [8, 128, 16], F),
    "xdo": ("dram", [128, 16], F), "xdi": ("dram", [8, 128, 16], F),
})
SCRATCH.update({n: ("psum", [128, 512], F) for n in "pb0 pb1 pb2 pa0 pa1 pa2".split()})
SEMAPHORES = ("v a t p ds dn0 dn1 de mo xo co yo lx lw lm lc".split()
              + [s + str(r) for s in ("x", "w", "m", "c", "ld", "lx", "lc") for r in range(8)])


def rank_program(g, core, T, topo):
    r = T.rank_of(core)
    if r is None:
        return
    cores = T.cores
    N = len(cores)
    V, A, P, Y = g.vector, g.scalar, g.tensor, g.sync
    eng = {"v": V, "a": A, "t": P, "p": g, "y": Y}
    cnt = {"v": 0, "a": 0, "t": 0, "p": 0}
    seen = {}
    nb = [d for d in (r + 1, r - 1) if 0 <= d < N]

    def wait(q, name, val):
        if val > seen.get((q, name), 0):
            seen[(q, name)] = val
            eng[q].wait_ge(T.sem[name], val)

    def do(q, fn, *deps):
        for name, val in deps:
            wait(q, name, val)
        fn().then_inc(T.sem[q], 1)
        cnt[q] += 1
        return (q, cnt[q])

    def ts(out, in0, s1, s2, op0, *op1, dep=()):
        return do("v", lambda: V.tensor_scalar(out, in0, s1, s2, op0, *op1), *dep)

    def tt(out, in0, in1, op, dep=()):
        return do("v", lambda: V.tensor_tensor(out, in0, in1, op), *dep)

    def cp(out, in_, dep=()):
        return do("v", lambda: V.tensor_copy(out, in_), *dep)

    def mm(out, lh, rh, start, stop, dep=()):
        return do("t", lambda: P.matmul(out, lh, rh, start, stop), *dep)

    def act(out, in_, func, dep=(), **kw):
        return do("a", lambda: A.activation(out, in_, func, **kw), *dep)

    def blk(buf, d):
        return buf[:, 256 * d:256 * d + 256]
    hf = [slice(0, 128), slice(128, 256)]
    slot = {r: 0}
    for d in nb:
        slot[d] = len(slot)

    for h in range(2):
        (Y, A)[h].dma_start(T.syi[0:1, 4 * h:4 * h + 4, :], T.sy[h::2, :]).then_inc(T.sem.ds, 16)
    for t in range(4):
        (Y, A)[t % 2].dma_start(T.nxi[:, 128 * t:128 * t + 128], T.nx[2 * t:2 * t + 2, :]).then_inc(T.sem["dn%d" % (t // 2)], 16)
    for t in range(4):
        (Y, A)[t % 2].dma_start(T.emi[:, 128 * t:128 * t + 128], T.em[2 * t:2 * t + 2, :]).then_inc(T.sem.de, 16)
    DS, DN, DE = ("ds", 32), [("dn0", 32), ("dn1", 32)], ("de", 64)

    def iota(ap, pattern, base, cm):
        return do("p", lambda: g.iota(ap, pattern, base, cm, allow_small_or_imprecise_dtypes=True))
    iota(T.ipi[:, 0:1], [[0, 1]], 0, 1)
    iota(T.ipf[:, 0:1], [[0, 1]], 0, 1)
    pq = iota(T.rm[:, 0:16], [[1, 16]], 0, 0)
    pc = iota(T.mi[:, :], [[1, 128]], 0, 0)
    pi2 = iota(T.io2[:, :], [[1, 256]], 0, 0)
    iota(T.mq[:, :], [[0, 8], [1, 16]], 0, 0)
    iota(T.mg[:, :], [[1, 8], [0, 16]], 0, 0)
    iota(T.iot[:, 0:32], [[1, 32]], 32 * r, 0)
    iota(T.iot[:, 32:64], [[1, 32]], 32 * r - 1, 0)
    iota(T.l2[:, 0:6], [[2, 6]], 0, 0)
    pio = iota(T.g8[:, :], [[0, 12], [1, 8]], 0, 0)
    pz = pio
    if r:
        pz = iota(T.big[:, 0:256 * r], [[0, 256 * r]], 0, 0)
    zeros = 256 * min(N, r + 2)
    pcz = iota(T.cnt[:, 0:zeros], [[0, zeros]], 0, 0)

    CB = 129
    BZ = 2047.0 - 4096 * CB
    von = do("v", lambda: V.memset(T.ones[:, :], 1.0))
    ts(T.qgi[:, 0:1], T.ipi[:, 0:1], 15, None, ALU.bitwise_and, dep=[pq])
    ts(T.qgi[:, 2:3], T.ipi[:, 0:1], 63, None, ALU.bitwise_and)
    v = ts(T.qgi[:, 1:2], T.ipi[:, 0:1], 4, None, ALU.logical_shift_right)
    qcol, gcol, pcol, m0 = T.qgf[:, 0:1], T.qgf[:, 1:2], T.ipf[:, 0:1], T.rm[:, 0:1]
    ts(T.hm[:, 0:1], pcol, 64.0, None, ALU.is_lt)
    ts(T.hm[:, 1:2], pcol, 64.0, None, ALU.is_ge)
    vqg = cp(T.qgf[:, 0:3], T.qgi[:, 0:3], dep=[v])
    vrm = ts(T.rm[:, :], T.rm[:, :], qcol, None, ALU.is_equal, dep=[vqg])
    vg16 = tt(T.qgf[:, 3:4], pcol, qcol, ALU.subtract)
    vbi = ts(T.bias[:, 0:16], T.rm[:, :], BZ, None, ALU.mult, dep=[vrm])
    vwx = ts(T.wx[:, :], T.mi[:, :], pcol, 4096.0, ALU.is_equal, ALU.mult, dep=[pc])
    v = ts(T.zw[:, :], T.mi[:, :], T.qgf[:, 3:4], 1.0 / 256, ALU.is_equal, ALU.mult, dep=[vg16])
    vzw = ts(T.zw0[:, :], T.zw[:, :], m0, None, ALU.mult, dep=[v])
    for seg in range(2):
        mm(T["pa%d" % seg][:, 0:128], T.ones[0:1, :], T.ones[0:1, :], True, False, dep=[von])
    for seg in range(2):
        vrow = cp(T.syr[0:1, seg:256:2], T.syi[0:1, :, 16 * seg:16 * seg + 16], dep=[DS])
    tbc = mm(T.pb0[:, 0:256], T.ones[0:1, :], T.syr[0:1, :], True, True, dep=[von, vrow])
    act(T.bias[:, 16:17], m0, ACTF.Copy, scale=float(128 * (2 * r + 1)), dep=[vrm])
    act(T.bias[:, 18:19], m0, ACTF.Copy, scale=-17 * CB / 256.0)
    act(T.cu[:, 0:1], m0, ACTF.Identity, scale=255.0, bias=1.0)
    act(T.cu[:, 1:2], m0, ACTF.Identity, scale=-255.0 / 256, bias=1.0)
    acu = act(T.cu[:, 2:3], m0, ACTF.Copy, scale=float(128 * (2 * r + 3)))
    aid = act(T.idw[:, :], T.io2[:, :], ACTF.Identity, scale=m0, bias=T.bias[:, 16:17], dep=[acu, pi2])

    def cast(h):
        return cp(T.nxh[:, 256 * h:256 * h + 256], T.nxi[:, 256 * h:256 * h + 256], dep=[DN[h]])
    vn = [cast(0)]
    for h in range(2):
        for seg in range(2):
            vsm = ts(T.selm[:, seg:8:2, 16 * h:16 * h + 16], T.pb0[:, 128 * h + seg:128 * h + 128:2], T.qgf[:, 2:3], T.hm[:, h:h + 1],
                     ALU.is_equal, ALU.mult, dep=[tbc])
    vn.append(cast(1))
    hs = [slice(0, 64), slice(64, 128)]
    for h in range(2):
        vsa = ts(T.sela[hs[h], :], T.pb0[hs[h], 128 * h:128 * h + 128], T.qgf[hs[h], 2:3], None, ALU.is_equal)
    vt = []
    for u in range(2):
        for h in range(2):
            v = ts(T.tb[:, 16 * u:16 * u + 16, 16 * h:16 * h + 16], T.nxh[:, 256 * u:256 * u + 256], T.hm[:, h:h + 1], None, ALU.mult,
                   dep=[vn[u]])
        vt.append(v)
    vem = ts(T.emh[:, :], T.emi[:, :], -2048, None, ALU.add, dep=[DE])

    for t in range(4):
        for seg in range(2):
            txn = mm(T.pb2[32 * t:32 * t + 32, hf[seg]], T.selm[:, 2 * t + seg, :], T.nxh[:, 128 * t:128 * t + 128],
                     True, True, dep=[vsm, vn[t // 2]])
    for t in range(4):
        for c in range(8):
            tof = mm(T.pb1[32 * t:32 * t + 32, c:256:8], T.tb[:, 8 * t + c, :], T.sela[:, 32 * t:32 * t + 32], True, True,
                     dep=[vt[t // 2], vsa])
    ac1 = act(T.c1[:, :], T.pb2[:, 0:256], ACTF.Copy, scale=1.0 / 128, bias=CB - 0.498, dep=[txn])
    tpx = []
    for seg in range(2):
        for t in range(4):
            mm(T["pa%d" % seg][32 * t:32 * t + 32, 0:128], T.selm[:, 2 * t + seg, :], T.emh[:, 128 * t:128 * t + 128], False, False,
               dep=[vem])
        tpx.append(mm(T["pa%d" % seg][:, 0:128], T.wx[:, :], T.c1[:, hf[seg]], False, True, dep=[vwx, ac1]))
    aa = {}
    for i in [15, 14, 13, 0, 12, 11, 10, 9, 8, 7, 6, 5, 4, 3, 2, 1]:
        for seg in range(2):
            o = T.ab[:, 256 * i + 128 * seg:256 * i + 128 * seg + 128] if i else T.xpb[:, hf[seg]]
            aa[i, seg] = act(o, T["pa%d" % seg][:, 0:128], ACTF.Identity, dep=[tpx[seg], vbi], scale=T.rm[:, i:i + 1],
                             bias=T.bias[:, i:i + 1])
    ax = aa[0, 1]

    vof = {}

    def lists(lo, hi, part):
        a, b = 16 * lo, 16 * hi
        if part == 0:
            vof["x"] = cp(T.oi[:, lo:hi, :], T.pb1[:, a:b], dep=[tof])
        elif part == 1:
            vof["x"] = ts(T.oi2[:, lo:hi, :], T.oi[:, lo:hi, :], 127, None, ALU.bitwise_and, dep=[vof["x"]])
        else:
            cp(T.off[:, lo:hi, 0:8], T.oi2[:, lo:hi, 0:8], dep=[vof["x"]])
            x = ts(T.off[:, lo:hi, 8:16], T.oi2[:, lo:hi, 8:16], 128, None, ALU.add)
            for i in range(lo, hi):
                vof[i] = x
    todo = [(lo, hi, part) for lo, hi in [(12, 16), (8, 12), (0, 8)] for part in range(3)]
    for _ in range(3):
        lists(*todo.pop(0))

    prev, vw = T.idw[:, :], aid
    for i in range(15, -1, -1):
        o = T["w%d" % (i % 2)][:, :] if i else blk(T.big, r)
        if i == 15:
            for seg in range(2):
                vw = tt(o[:, hf[seg]], prev.indirect(T.off[:, i, 8 * seg:8 * seg + 8]),
                        T.ab[:, 256 * i + 128 * seg:256 * i + 128 * seg + 128], ALU.add, dep=[vof[i], aid, aa[i, seg]])
        elif i:
            vw = tt(o, prev.indirect(T.off[:, i, :]), T.ab[:, 256 * i:256 * i + 256], ALU.add, dep=[vof[i], vw, aa[i, 1]])
        else:
            vw = cp(o, prev.indirect(T.off[:, i, :]), dep=[vof[i], vw])
        prev = o
        if todo:
            lists(*todo.pop(0))
    vu = ts(T.uo[:, :], blk(T.big, r), T.bias[:, 16:17], T.cu[:, 0:1], ALU.subtract, ALU.mult, dep=[vw, acu])
    pcn = T.pa2[:, 0:256]
    mm(pcn, T.zw0[:, :], T.c1[:, :], True, False, dep=[vzw])
    acc = act(T.cc[:, :], blk(T.big, r), ACTF.Copy, scale=1.0 / 4096, bias=CB - 0.5 + 1.0 / 8192, dep=[vw])
    tcn = mm(pcn, T.zw[:, :], T.cc[:, :], False, True, dep=[acc])
    acn = act(blk(T.cnt, r), pcn, ACTF.Identity, bias=T.bias[:, 18:19], dep=[tcn, pcz, acu])
    apy = act(blk(T.pay, 0), blk(T.big, r), ACTF.Copy)

    def send(buf_src, buf_dst, sem, lsem, dests):
        mask = topo.mask(core, cores[dests[0]])
        ids = []
        for d in dests:
            rid, pid = topo.addr(cores[d], core)
            ids.append(DstId(rid=rid, pnc=pid))
        g.remote_dma_fused([RemoteDMATransfer(dst_ids=ids, dma_engine_mask=mask, remote_sem=T.sem[sem],
                                              srcs=[buf_src], dsts=[buf_dst] * len(ids))], local_sem=T.sem[lsem])
        return len(topo.engines(core, cores[dests[0]]))
    wait("y", *ax)
    Y.dma_start(T.xdo[:, :], T.xpb[0:128:16, :]).then_inc(T.sem.xo, 16)
    wait("p", "xo", 16)
    ne = send(T.xdo[:, :], T.xdi[r], "x%d" % r, "lx", nb)
    wait("p", *vu)
    send(T.uo[:, :], blk(T.ui, r), "w%d" % r, "lw", nb)
    far = list(range(N - 1, r, -1))
    if far:
        wait("y", *vw)
        Y.dma_start(T.mdo[:, :], blk(T.big, r)[0:128:16, :]).then_inc(T.sem.mo, 16)
        wait("p", "mo", 16)
        send(T.mdo[:, :], T.mdi[r], "m%d" % r, "lm", far)
    wait("y", *acn)
    Y.dma_start(T.cdo[:, :], blk(T.cnt, r)[0:128:16, :]).then_inc(T.sem.co, 16)
    wait("p", "co", 16)
    send(T.cdo[:, :], T.cdi[r], "c%d" % r, "lc", far + ([r - 1] if r else []))
    wait("a", "xo", 16)
    wait("a", *apy)
    A.dma_start(blk(T.pay, 0)[0:128:16, :], T.xdo[:, :]).then_inc(T.sem["lx%d" % r], 16)
    for d in range(r):
        qn = "ya"[d % 2]
        wait(qn, *pz)
        wait(qn, "m%d" % d, ne)
        eng[qn].dma_start(blk(T.big, d)[0:128:16, :], T.mdi[d]).then_inc(T.sem["ld%d" % d], 16)

    kmin, kmax = max(0, 2 * r - 2), min(2 * N - 1, 2 * r + 3)
    nk = kmax - kmin + 1
    do("v", lambda: V.memset(T.s[:, :], 0))
    ts(T.pfx[:, 0:32], T.io2[:, 0:32], 0.0, None, ALU.mult)
    vsg = ts(T.sg[:, :], T.mg[:, :], gcol, None, ALU.is_equal, dep=[pio])
    v = ts(T.tri0[:, :], T.mq[:, :], qcol, None, ALU.is_gt)
    tt(T.tri[:, :], T.tri0[:, :], T.sg[:, :], ALU.mult, dep=[v, vsg])
    ts(T.wb[:, :], T.sg[:, :], m0, 256.0, ALU.mult, ALU.mult)
    v = ts(T.n0[:, 2:3], qcol, 8.0, None, ALU.is_ge)
    ts(T.gl[:, 0:6], T.l2[:, 0:6], T.n0[:, 2:3], None, ALU.add, dep=[v, pio])
    vcn = ts(T.gsr[:, :], T.g8[:, :], gcol, None, ALU.is_equal)

    for e in nb:
        wait("y", "x%d" % e, ne)
        wait("y", *cp(blk(T.pay, slot[e]), blk(T.ui, e), dep=[("w%d" % e, ne)]))
        Y.dma_start(blk(T.pay, slot[e])[0:128:16, :], T.xdi[e]).then_inc(T.sem["lx%d" % e], 16)
        if e > r:
            vcv = ts(blk(T.big, e), blk(T.ui, e), T.cu[:, 1:2], T.cu[:, 2:3], ALU.mult, ALU.add, dep=[acu])
    cin = [d for d in range(min(N, r + 2)) if d != r]
    for d in cin:
        wait("y", *pcz)
        wait("y", "c%d" % d, ne)
        Y.dma_start(blk(T.cnt, d)[0:128:16, :], T.cdi[d]).then_inc(T.sem["lc%d" % d], 16)

    vs = vcn
    wait("v", *pz)
    ka = max(0, kmax - 5)
    for k in range(kmax + 1):
        if k in (ka, kmax) and k:
            a = 0 if k == ka else ka
            b = a + a % 2
            v = cp(T.lsc[:, b:b + k - a], T.s[:, 2 * a:2 * k:2], dep=[vs])
            acf = act(T.cf[:, 16 * a:16 * k], T.cnt[:, 0:zeros].indirect(T.lsc[:, b:b + k - a]), ACTF.Copy, scale=m0,
                      dep=[v, acn, pcz] + [("lc%d" % d, 16) for d in cin])
        if k == kmax:
            break
        d = k // 2
        win = T.big[:, 0:256 * d + 256]
        off = T.s[:, 2 * k:2 * k + 1]
        vs = ts(T.s[:, 2 * k + 2:2 * k + 18], win.indirect(off), m0, None, ALU.mult,
                dep=[vs] + ([("ld%d" % d, 16)] if d < r else [vw]) + ([vcv] if d > r else []))
    kl = 2 if r else 0
    if r:
        ts(T.lst[:, 0:2], T.s[:, 2 * kmin:2 * kmin + 4:2], 256 * (slot[r - 1] - (r - 1)), None, ALU.add, dep=[vs])
    vl = ts(T.lst[:, kl:nk], T.s[:, 2 * (kmin + kl):2 * (kmin + nk):2], -256 * r, None, ALU.add, dep=[vs])
    lst = T.lst[:, 0:nk]
    m = 16 * nk
    v2 = cp(T.v2[:, 0:m], T.pay[:, 0:256 * len(slot)].indirect(lst), dep=[vl] + [("lx%d" % d, 16) for d in slot])
    vv = T.v2[:, 0:m:16]
    ts(T.cab[:, 0:nk], vv, 4096, None, ALU.is_ge, dep=[v2])
    vca = ts(T.cab[:, nk:2 * nk], vv, 8192, None, ALU.is_ge)
    ts(T.ei[:, 0:nk], vv, 63, None, ALU.bitwise_and)
    ve = ts(T.ei[:, nk:2 * nk], vv, 6, 63, ALU.logical_shift_right, ALU.bitwise_and)
    vpx = do("v", lambda: V.tensor_tensor_scan(T.pfx[:, 1:1 + kmax], T.cf[:, 0:16 * kmax:16], T.cf[:, 0:16 * kmax:16], 0.0, ALU.add, ALU.max),
             acf)
    pp = T.pb1[:, 0:nk]
    mm(pp, T.tri[:, :], T.cab[:, 0:nk], True, False, dep=[vca, vcn])
    mm(pp, T.tri[:, :], T.cab[:, nk:2 * nk], False, False)
    tp = mm(pp, T.wb[:, :], T.pfx[:, kmin:kmax + 1], False, True, dep=[vpx])

    vo = {}

    def onehot(kk):
        vo[kk] = ts(T.oh[:, 64 * kk:64 * kk + 64], T.iot[:, :], T.pb1[:, kk:kk + 1], None, ALU.is_equal, dep=[tp])
    v = ts(T.ef[:, 0:2 * nk], T.ei[:, 0:2 * nk], 1, None, ALU.add, dep=[ve])
    v = tt(T.val[:, 0:2 * nk], T.ef[:, 0:2 * nk], T.cab[:, 0:2 * nk], ALU.mult, dep=[v])
    vgv = tt(T.gsv[:, 0:m], T.val[:, 0:2 * nk].indirect(T.gl[:, 0:nk]), T.gsr[:, 0:m], ALU.mult, dep=[v])
    yp = T.pb2[0:8, 0:32]
    for kk in range(nk):
        onehot(kk)
        for mh in range(2):
            x = mh * nk + kk
            ty = mm(yp, T.gsv[:, 8 * x:8 * x + 8], T.oh[:, 64 * kk + 32 * mh:64 * kk + 32 * mh + 32], kk + mh == 0, kk + mh == nk,
                    dep=[vo[kk], vgv])
    vy = ts(T.ys[0:8, :], yp, -1.0, None, ALU.add, dep=[ty])
    wait("y", *vy)
    Y.dma_start(T.y[:, :], T.ys[0:8, :]).then_inc(T.sem.yo, 16)

    wait("y", "yo", 16)
    wait("p", "lx", ne)
    wait("p", "lw", ne)
    wait("p", "lc", ne)
    if far:
        wait("p", "lm", ne)
    for name in ("v", "a", "t"):
        wait("p", name, cnt[name])
    wait("v", "p", cnt["p"])
